import numpy as np, ml_dtypes
CORES = [5,29,101,125,133,157,229,253]
N = 8
BF = ml_dtypes.bfloat16
W, RO, F, INV = 2016, 3, 2, 0
def rises(g):
    return np.sum(g > np.arange(W), axis=-1)
def perms(rng, *shape):
    return np.argsort(rng.random(shape + (W,)), axis=-1)
def some(rng, m):
    a = np.arange(W); s = rng.permutation(W)[:m]; a[s] = rng.permutation(s)
    return a
def turned(p):
    return W - 1 - np.argsort(p)[::-1]
def lower(rng, p):
    a = np.arange(W); b = np.argsort(p); v = int(rng.choice(np.flatnonzero((p > a) & (b < a))))
    q = p.copy(); q[b[v]] = p[v]; q[v] = v
    return q
def pack(g):
    return {"g0": np.ascontiguousarray(g.reshape(N, 128, W)).astype(np.int32)}
def setup_inputs(rng):
    g = perms(rng, N, 8, 16); part = rng.random((N, 8, 16)) < 0.4
    for q, k, i in np.argwhere(part):
        g[q, k, i] = some(rng, int(W * (0.3 + 0.7 * rng.random())))
    return pack(g)
def setup_inputs_ties(rng):
    g = perms(rng, N, 8, 16)
    for k in range(4):
        b = int(rng.integers(1, 9)); o = rng.permutation(W); pr = o[:2 * b].reshape(b, 2); rings = [np.sort(x) for x in np.array_split(o[2 * b:], b)]
        for q in range(N):
            top = int(rng.integers(0, 16))
            for i in range(16):
                if i != top and rng.random() < 0.2: continue
                a = np.arange(W); swap = i == top or rng.random() < 0.5
                for s in rings: a[s] = np.roll(s, -1 if i == top else -int(rng.integers(2, 61)))
                if swap: a[pr[:, 0]] = pr[:, 1]; a[pr[:, 1]] = pr[:, 0]
                g[q, k, i] = a
    for k in range(4, 8):
        for q in range(N):
            j = int(np.argmax(rises(g[q, k]))); i = (j + int(rng.integers(1, 16))) % 16
            g[q, k, i] = turned(g[q, k, j])
    return pack(g)
def setup_inputs_ends(rng):
    a = np.arange(W); x = a.copy(); x[0] = W - 1; x[W - 1] = 0
    kinds = np.stack([a, a[::-1], np.roll(a, -1), np.roll(a, 1), x]); p = perms(rng, N, 8, 16)
    g = np.where((rng.random((N, 8, 16)) < 0.4)[..., None], p, kinds[rng.integers(0, 5, (N, 8, 16))])
    o = rng.permutation(8)
    g[:, o[0]] = a
    g[:, o[1]] = p[:, o[1]]; g[rng.integers(0, N), o[1]] = a
    g[:, o[2]] = p[:, o[2]]; g[::2, o[2], 15] = kinds[2]; g[1::2, o[2], 0] = kinds[2]
    g[:, o[3]] = p[:, o[3]]
    for q in range(N):
        m = g[q, o[3]].copy(); j = int(np.argmax(rises(m)))
        if q % 2 == 0:
            m[[j, 15]] = m[[15, j]]; c = int(rises(m[15])); m[0] = lower(rng, turned(m[15]))
            for i in range(1, 15):
                if int(rises(m[i])) == c: m[i] = lower(rng, m[i])
        else:
            m[[0, j]] = m[[j, 0]]; u = int(np.argmax(m[0])); w = int(m[0, W - 2]); m[0, u] = w; m[0, W - 2] = W - 1
            m[1] = turned(m[0]); y = m[1].copy()
            s = np.flatnonzero((a < W // 2) & (y >= W // 2)); y[s] = y[rng.permutation(s)]
            m[int(rng.integers(2, 16))] = y
        g[q, o[3]] = m
    return pack(g)
def setup_inputs_grow(rng):
    g = np.zeros((N, 8, 16, W), np.int64); m = np.exp2(1 + (np.log2(W) - 3) * rng.random((N, 8, 16))).astype(np.int64)
    for q, k, i in np.ndindex(N, 8, 16): g[q, k, i] = some(rng, int(m[q, k, i]))
    return pack(g)
def setup_inputs_alike(rng):
    p = perms(rng, N, 8, 3); p[:, :3] = p[0, :3].copy(); p[:, :, 2] = np.argsort(p[:, :, 1], axis=-1)
    g = np.take_along_axis(p, rng.integers(0, 3, (N, 8, 16))[..., None], 2)
    g[:, 7] = g[:, 7, :1].copy()
    h = W // 2 - 1
    for q in range(N):
        o = rng.permutation(W); s = np.sort(o[:h]); z = np.sort(o[h:2 * h])
        a = np.arange(W); a[s] = np.roll(s, -1); a[z] = np.roll(z, 1); b = some(rng, W // 8)
        k = rng.integers(0, 3, 16); k[rng.integers(0, 16)] = 0
        g[q, 5] = np.stack([a, b, np.argsort(b)])[k]
    o = 1 + rng.permutation(W - 3); m = W // 2
    up = np.sort(np.append(o[:m - 2], [0, W - 2])); down = np.sort(np.append(o[m - 2:], [W - 1]))[::-1]; nxt = np.roll(down, -1)
    one = np.zeros(W, np.int64); one[up] = down; one[down] = up
    two = np.zeros(W, np.int64); two[up] = nxt; two[nxt] = up
    r = int(rng.integers(0, N)); g[:, 6] = np.roll(np.arange(W), -1); g[r, 6] = one; g[(r + 1 + F) % N, 6] = two
    return pack(g)
def setup_inputs_spread(rng):
    g = np.zeros((N, 8, 16, W), np.int64)
    for q, k, i in np.ndindex(N, 8, 16):
        m = max(2, min(W, int(np.exp2(1 + (np.log2(W) - 1) * rng.random()) + 0.5)))
        if rng.random() < 0.5:
            s = np.sort(rng.permutation(W)[:m]); u = rng.random(); a = np.arange(W); a[s] = np.roll(s, -min(m - 1, 1 + int((m - 1) * u * u * u))); g[q, k, i] = a
        else: g[q, k, i] = some(rng, m)
    return pack(g)
def check_inputs(d):
    a = np.asarray(d["g0"])
    if a.shape != (N, 128, W) or np.any(np.sort(a, axis=-1) != np.arange(W)): return ["rows of g0 are permutations"]
    return []
def reference(g0):
    g = g0.astype(np.int64).reshape(N, 8, 16, W); e = rises(g)
    for t in range(RO):
        J = np.argmax(e, axis=2)
        L = np.take_along_axis(g, J[:, :, None, None], 2)
        for s in range(F + 1):
            if s == 0: M = L
            else: M = L[np.array([(r + 1 + (t * F + s - 1) % (N - 1)) % N for r in range(N)])]
            ix = np.broadcast_to(M, g.shape)
            if s > 0 and INV:
                h = np.zeros_like(g); np.put_along_axis(h, ix, g, 3)
            else: h = np.take_along_axis(g, ix, 3)
            eh = rises(h); up = eh > e
            g = np.where(up[..., None], h, g); e = np.where(up, eh, e)
    return {"yg": g.reshape(N, 128, W).astype(np.float32), "ye": e.reshape(N, 128, 1).astype(np.float32)}

@@ -1,0 +1,417 @@
+from concourse.mybir import AluOpType as Op, AxisListType, ActivationFunctionType as Act
+
+W, RO, F, N = 2016, 3, 2, 8
+K = W // 16
+CB = [0, 448, 832, 1344, 1728, 2016]
+NC = len(CB) - 1
+SC = (0, 2)
+HM = (0,)
+HALF = CB[2]
+SPARE = 2
+BIG = 30000.0
+LOADS = [(0, 1), (1, 2), (2, 4), (4, 5)]
+STORES = [(4, 5), (2, 4), (0, 2)]
+VT = CB[1]
+PB2 = 4
+ORDP = (1, 2, 3, 0, 4)
+ORDL = (4, 2, 3, 0, 1)
+ORDV = (0, 2, 1, 3, 4)
+ORDG = (1, 2, 3, 4)
+
+SCRATCH = {
+    "gi": ("sbuf", [128, W], "int32"),
+    "p32": ("sbuf", [128, W], "float32"),
+    "p16": ("sbuf", [128, W], "float16"),
+    "dl": ("sbuf", [128, W], "float16"),
+    "v16": ("sbuf", [128, W], "float16"),
+    "junk": ("sbuf", [128, W], "bfloat16"),
+    "h32": ("sbuf", [128, CB[1]], "float32"),
+    "jj": ("sbuf", [128, 256], "float32"),
+    "j16": ("sbuf", [128, 128], "float32"),
+    "pint": ("sbuf", [128, 2], "int32"),
+    "col": ("sbuf", [128, 16], "float32"),
+    "acc": ("sbuf", [128, 8 * (3 * RO + 2)], "float32"),
+    "ecol": ("sbuf", [128, 1], "float32"),
+    "eye": ("sbuf", [128, 128], "float16"),
+    "neye": ("sbuf", [128, 128], "float16"),
+    "ipos": ("sbuf", [128, 128], "float16"),
+    "ineg": ("sbuf", [128, 128], "float16"),
+    "keep": ("sbuf", [128, 128], "float16"),
+    "take": ("sbuf", [128, 128], "float16"),
+    "grp": ("sbuf", [128, 128], "float16"),
+    "rm": ("sbuf", [128, 16], "float16"),
+    "rtb": ("sbuf", [128, 16], "float16"),
+    "rr": ("sbuf", [128, 16], "float16"),
+    "cb0": ("sbuf", [128, 144], "float16"),
+    "cb": ("sbuf", [128, 144], "float16"),
+    "sel": ("sbuf", [128, 144], "float16"),
+    "pe": ("psum", [128, 512], "float32"),
+}
+for _j in range(NC):
+    SCRATCH["pa%d" % _j] = ("psum", [128, 512], "float32")
+for _j in SC:
+    SCRATCH["pb%d" % _j] = ("psum", [128, 512], "float32")
+for _t in range(RO):
+    for _n in ("own", "hand", "m1_", "m2_"):
+        SCRATCH["%s%d" % (_n, _t)] = ("sbuf", [128, K], "uint16")
+
+SEMAPHORES = (["cv", "cs", "ct", "cg", "st", "ste", "sent"] + ["ld%d" % k for k in range(len(LOADS))]
+              + ["%s%d" % (n, t) for t in range(RO) for n in ("hand", "m1_", "m2_")])
+
+
+def route(T, topo, r, t, s):
+    src = T.cores[r]
+    dst = T.cores[(r - 1 - (F * t + s - 1) % (N - 1)) % N]
+    if topo.may_write(src, dst):
+        return dst, None
+    able = [c for c in topo.cores_of(src) if T.rank_of(c) is None and topo.may_write(c, dst)]
+    near = [c for c in able if topo.die(c) == topo.die(src)]
+    return dst, (near or able)[0]
+
+
+def arrivals(T, topo, r, t, s):
+    q = (r + 1 + (F * t + s - 1) % (N - 1)) % N
+    dst, via = route(T, topo, q, t, s)
+    return len(topo.engines(T.cores[q] if via is None else via, dst))
+
+
+def narrow(T, topo, core):
+    far = [c for c in T.cores if c != core and topo.may_write(core, c)]
+    return topo.mask(core, far[0]), len(topo.engines(core, far[0]))
+
+
+def relay_program(g, core, T, topo):
+    sent = 0
+    for t in range(RO):
+        for s in range(1, F + 1):
+            for r in range(N):
+                dst, via = route(T, topo, r, t, s)
+                if via != core:
+                    continue
+                g.wait_ge(T.sem["hand%d" % t], narrow(T, topo, T.cores[r])[1])
+                rid, pid = topo.addr(dst, core)
+                g.remote_dma(T["m%d_%d" % (s, t)][:], T["hand%d" % t][:], T.sem["m%d_%d" % (s, t)], T.sem.sent,
+                             pid, rid, topo.mask(core, dst))
+                sent += len(topo.engines(core, dst))
+    if sent:
+        g.wait_ge(T.sem.sent, sent)
+
+
+def emit(g, T, ops, ext):
+    queues = {"v": g.vector, "s": g.scalar, "t": g.tensor, "g": g, "y": g.sync}
+    writer, readers, known, clock, waits, needed = {}, {}, {q: {} for q in queues}, [], [], set()
+    chain = lambda i: ops[i][4] or "c" + ops[i][0]
+    for i, (q, call, rd, wr, dma) in enumerate(ops):
+        deps = set(writer[k] for k in rd + wr if k in writer)
+        for k in wr:
+            deps.update(readers.get(k, []))
+        mine = []
+        for k in rd:
+            if k in ext and ext[k][0] not in known[q]:
+                known[q][ext[k][0]] = 0
+                mine.append(ext[k])
+        for d in sorted(deps, reverse=True):
+            if q == "t" and ops[d][0] == "t":
+                continue
+            if known[q].get(chain(d), -1) >= d:
+                continue
+            needed.add(d)
+            mine.append(d)
+            for c, x in clock[d].items():
+                known[q][c] = max(known[q].get(c, -1), x)
+        waits.append(mine)
+        mark = dict(known[q])
+        mark[chain(i)] = i
+        clock.append(mark)
+        for k in wr:
+            writer[k] = i
+            readers[k] = []
+        for k in rd:
+            readers.setdefault(k, []).append(i)
+    count, value = {}, {}
+    for i, (q, call, rd, wr, dma) in enumerate(ops):
+        for d in waits[i]:
+            if isinstance(d, tuple):
+                queues[q].wait_ge(T.sem[d[0]], d[1])
+            else:
+                queues[q].wait_ge(T.sem[chain(d)], value[d])
+        ins = call()
+        if dma == "sent":
+            continue
+        if dma or i in needed:
+            n = 16 if dma else 1
+            count[chain(i)] = value[i] = count.get(chain(i), 0) + n
+            ins.then_inc(T.sem[chain(i)], n)
+    return count
+
+
+def rank_program(g, core, T, topo):
+    rank = T.rank_of(core)
+    if rank is None:
+        relay_program(g, core, T, topo)
+        return
+    V, S, PE = g.vector, g.scalar, g.tensor
+    X = AxisListType.X
+    ops = []
+    ext = {"m%d_%d" % (s, t): ("m%d_%d" % (s, t), arrivals(T, topo, rank, t, s))
+           for t in range(RO) for s in range(1, F + 1)}
+    emask, en = narrow(T, topo, core)
+    every = lambda n: ["%s%d" % (n, j) for j in range(NC)]
+    cols = lambda j: slice(CB[j], CB[j + 1])
+    bank = lambda n, j: T["%s%d" % (n, j)][:, 0:CB[j + 1] - CB[j]]
+    col = lambda k: T.col[:, k:k + 1]
+    acc = lambda k, a, b=None: T.acc[:, 8 * k + a:8 * k + (a + 1 if b is None else b)]
+
+    def op(q, rd, wr, fn, *args, dma=None, **kw):
+        ops.append((q, lambda: fn(*args, **kw), list(rd), list(wr), dma))
+
+    def ts(rd, wr, out, in0, s1, s2, o0, o1=None):
+        if o1 is None:
+            op("v", rd, wr, V.tensor_scalar, out, in0, s1, None, o0)
+        else:
+            op("v", rd, wr, V.tensor_scalar, out, in0, s1, s2, o0, o1)
+
+    def mm(n, j, lhs, rhs, start=False, stop=False):
+        op("t", [lhs, "%s%d" % (rhs, j)], ["%s%d" % (n, j)], PE.matmul, bank(n, j), T[lhs][:], T[rhs][:, cols(j)],
+           start, stop)
+
+    def count(k, j, place):
+        op("s", [], ["pa%d" % j, "junk%d" % j, "acc%d_%d" % (k, place)], S.activation, T.junk[:, cols(j)],
+           bank("pa", j), Act.Sign, bias=-0.5, scale=-1.0, accum_out=acc(k, place))
+
+    def spot(t, h):
+        if h == 0:
+            return "pa%d" % SPARE, T["pa%d" % SPARE][:, 0:HALF // 16]
+        return "pe", T.pe[:, 16:16 + (W - HALF) // 16]
+
+    for k, (a, b) in enumerate(LOADS):
+        q, eng = (("s", S) if k == 1 else ("y", g.sync))
+        op(q, [], ["gi%d" % j for j in range(a, b)], eng.dma_start, T.gi[:, CB[a]:CB[b]], T.g0[:, CB[a]:CB[b]],
+           dma="ld%d" % k)
+    op("g", [], ["jj"], g.iota, T.jj[:], [[1, 256]], 0, 0, allow_small_or_imprecise_dtypes=True)
+    op("g", [], ["pint0"], g.iota, T.pint[:, 0:1], [[0, 1]], 0, 1)
+    op("g", [], ["j16"], g.iota, T.j16[:], [[16, 8], [0, 16]], 0, 0, allow_small_or_imprecise_dtypes=True)
+    PF, PM, PG, PG15, TB, THR, NPART, MN = range(8)
+    J = T.jj[:, 0:128]
+    op("v", ["jj"], ["va"], V.tensor_copy, T.v16[:, 0:256], T.jj[:])
+    ts(["jj"], ["vb"], T.v16[:, 256:512], T.jj[:], 256.0, None, Op.add)
+    op("v", ["pint0"], ["pf"], V.tensor_copy, col(PF), T.pint[:, 0:1])
+    ts(["pint0"], ["pint1"], T.pint[:, 1:2], T.pint[:, 0:1], 15, None, Op.bitwise_and)
+    ts(["va", "vb"], ["v160", "v161"], T.v16[:, 512:1024], T.v16[:, 0:512], 512.0, None, Op.add)
+    ts(["jj", "pf"], ["eye"], T.eye[:], J, col(PF), None, Op.is_equal)
+    ts(["jj", "pf"], ["neye"], T.neye[:], J, col(PF), -1.0, Op.is_equal, Op.mult)
+    op("v", ["pint1"], ["pm"], V.tensor_copy, col(PM), T.pint[:, 1:2])
+    ts(["v161"], ["v162", "v163", "v164"], T.v16[:, 1024:W], T.v16[:, 0:W - 1024], 1024.0, None, Op.add)
+    ts(["pf", "pm"], ["pg"], col(PG), col(PF), col(PM), None, Op.subtract)
+    ts(["pf", "pm"], ["pg15"], col(PG15), col(PF), col(PM), 15.0, Op.subtract, Op.add)
+    ts(["pm"], ["tb"], col(TB), col(PM), 0.125, None, Op.mult)
+    ts(["jj", "pm"], ["rm"], T.rm[:], T.jj[:, 0:16], col(PM), None, Op.is_equal)
+    late = [
+        lambda: ts(["j16", "pg"], ["grp"], T.grp[:], T.j16[:], col(PG), None, Op.is_equal),
+        lambda: ts(["jj", "pg15"], ["cb0"], T.cb0[:], T.jj[:, 0:144], col(PG15), BIG, Op.not_equal, Op.mult),
+        lambda: ts(["jj", "pm", "tb"], ["rtb"], T.rtb[:], T.jj[:, 0:16], col(PM), col(TB), Op.is_equal, Op.mult),
+        lambda: ts(["cb0", "tb"], ["cb"], T.cb[:], T.cb0[:], col(TB), None, Op.add),
+        lambda: ts(["jj", "pf"], ["ipos"], T.ipos[:], J, col(PF), BIG, Op.not_equal, Op.mult),
+        lambda: ts(["jj", "pf"], ["ineg"], T.ineg[:], J, col(PF), -BIG, Op.not_equal, Op.mult),
+    ]
+
+    def ties():
+        op("t", ["grp", "rtb"], ["pe"], PE.matmul, T.pe[:, 0:16], T.grp[:], T.rtb[:], True, False)
+
+    def spread(k):
+        ts(["rm", "acc%d_4" % k], ["rr"], T.rr[:], T.rm[:], acc(k, 4), None, Op.mult)
+
+    def side_by_side():
+        op("t", ["grp", "rr"], ["pe"], PE.matmul, T.pe[:, 0:16], T.grp[:], T.rr[:], False, True)
+
+    def choose(k):
+        op("v", [], ["pe", "mn"], V.tensor_reduce, col(MN), T.pe[:, 0:16], X, Op.min)
+        ts(["cb", "mn", "acc%d_4" % k], ["sel"], T.sel[:], T.cb[:], acc(k, 4), col(MN), Op.add, Op.is_le)
+
+    def lay(t, h):
+        lo, hi = (0, HALF) if h == 0 else (HALF, W)
+        src = ["p16%d" % j for j in range(NC) if lo <= CB[j] < hi]
+        key, out = spot(t, h)
+        for a in range(16):
+            op("t", ["sel"] + src, [key], PE.matmul, out, T.sel[:, 15 - a:143 - a], T.p16[:, lo + a:hi:16],
+               a == 0, a == 15)
+
+    def publish(t, h):
+        own = T["own%d" % t]
+        lo, hi = (0, HALF // 16) if h == 0 else (HALF // 16, K)
+        key, src = spot(t, h)
+        op("v", [], [key, "own%d_%d" % (t, h)], V.tensor_copy, own[:, lo:hi], src)
+        for s in (range(1, F + 1) if h == 1 else []):
+            dst, via = route(T, topo, rank, t, s)
+            to, name = (dst, "m%d_%d" % (s, t)) if via is None else (via, "hand%d" % t)
+            rid, pid = topo.addr(to, core)
+            op("g", ["own%d_0" % t, "own%d_1" % t], [], g.remote_dma, T[name][:], own[:], T.sem[name], T.sem.sent,
+               pid, rid, emask, dma="sent")
+
+    def ahead(j):
+        mm("pa", j, "eye", "v16", True)
+
+    def minus_p(j):
+        if j not in HM:
+            mm("pa", j, "neye", "p16")
+
+    for j in range(NC):
+        ahead(j)
+    for j in range(NC):
+        op("v", ["gi%d" % j], ["p16%d" % j], V.tensor_copy, T.p16[:, cols(j)], T.gi[:, cols(j)])
+        mm("pa", j, "neye", "p16", False, True)
+        count(0, j, j)
+        if j < 2:
+            for f in late[3 * j:3 * j + 3]:
+                f()
+        if j == 2:
+            ties()
+            ahead(0)
+        if j == 4:
+            ahead(1)
+            minus_p(1)
+    op("v", ["acc0_%d" % j for j in range(NC)], ["acc1_4"], V.tensor_reduce, acc(1, 4), acc(0, 0, NC), X, Op.add,
+       negate=True)
+    spread(1)
+    side_by_side()
+    choose(1)
+    lay(0, 0)
+    lay(0, 1)
+
+    for t in range(RO):
+        for s in range(F + 1):
+            k = 3 * t + s + 1
+            last = t == RO - 1 and s == F
+            turn = s == F and not last
+            win = "gi" if k == 1 else "p32"
+            lst = "own%d" % t if s == 0 else "m%d_%d" % (s, t)
+
+            def picked(a, b):
+                return T[win][:, 0:W].indirect(T[lst][:, a // 16:b // 16])
+
+            def name(a):
+                return lst if s else "%s_%d" % (lst, int(a >= HALF))
+
+            def gather(j, a, b):
+                if j in HM:
+                    op("v", every(win) + [name(a)], ["dl%d" % j], V.tensor_copy, T.dl[:, a:b], picked(a, b))
+                else:
+                    op("v", every(win) + [name(a), "p16%d" % j], ["dl%d" % j], V.tensor_tensor, T.dl[:, a:b],
+                       picked(a, b), T.p16[:, a:b], Op.subtract)
+
+            def held(j):
+                return "pb" if j in SC else "pa"
+
+            def before(j):
+                if j not in HM:
+                    mm(held(j), j, "eye", "p16", True)
+
+            def after(j):
+                if j in HM:
+                    op("t", ["keep", "p16%d" % j, "p16x"], ["%s%d" % (held(j), j)], PE.matmul, bank(held(j), j),
+                       T.keep[:], T.p16[:, cols(j)], True, False)
+                mm(held(j), j, "take", "dl", not (j in HM or j in SC or turn), True)
+
+            order = [0, 1, 2, 3, 4] if k == 1 else [1, 0, 2, 3, 4]
+            if s == 0:
+                publish(t, 0)
+            if k > 1:
+                op("s", every(win) + [name(0)], ["h32"], S.activation, T.h32[:], picked(0, CB[1]), Act.Copy)
+            for j in order:
+                if s == 0 and j >= 2:
+                    ahead(j)
+                if not (k == 1 and j == 1):
+                    minus_p(j)
+                if j == order[0] and s == 0:
+                    mid = (CB[j] + CB[j + 1]) // 64 * 32
+                    gather(j, CB[j], mid)
+                    publish(t, 1)
+                    gather(j, mid, CB[j + 1])
+                elif j == 0:
+                    op("v", ["h32"], ["dl0"], V.tensor_copy, T.dl[:, cols(0)], T.h32[:])
+                else:
+                    gather(j, CB[j], CB[j + 1])
+                mm("pa", j, "neye", "dl", False, True)
+                count(k, j, j if j < NC - 1 else 5)
+                if j == PB2:
+                    before(2)
+                if turn and j == 3:
+                    before(1)
+                    ties()
+                if turn and j == 4:
+                    before(3)
+            if s:
+                op("v", ["p320"], ["p160"], V.tensor_copy, T.p16[:, 0:VT], T.p32[:, 0:VT])
+            a4 = ["acc%d_%d" % (k, j) for j in range(4)]
+            ns, fin = "acc%d_4" % k, "acc%d_5" % k
+            op("v", a4 + [ns], ["thr"], V.tensor_reduce, col(THR), acc(k, 0, 5), X, Op.add, negate=True)
+            op("v", a4, ["npart"], V.tensor_reduce, col(NPART), acc(k, 0, 4), X, Op.add, negate=True)
+            ts(["ineg", fin, "thr"], ["take"], T.take[:], T.ineg[:], acc(k, 5), col(THR), Op.add, Op.is_gt)
+            ts(["ipos", fin, "thr"], ["keep"], T.keep[:], T.ipos[:], acc(k, 5), col(THR), Op.add, Op.is_le)
+            ts(["npart", fin, ns], ["acc%d_4" % (k + 1)], acc(k + 1, 4), col(NPART), acc(k, 5), acc(k, 4),
+               Op.subtract, Op.min)
+
+            if not turn:
+                if last:
+                    ts(["acc%d_4" % (k + 1)], ["ecol"], T.ecol[:], acc(k + 1, 4), -0.5, W / 2, Op.mult, Op.add)
+                    op("g", ["ecol"], [], g.dma_start, T.ye[:], T.ecol[:], dma="ste", allow_slow_non_contiguous=True)
+                for j in (ORDL if last else ORDP):
+                    after(j)
+                    if j in SC:
+                        op("s", [], ["pb%d" % j, "p32%d" % j], S.activation, T.p32[:, cols(j)], bank("pb", j), Act.Copy)
+                    elif j in HM:
+                        op("v", [], ["pa%d" % j, "p32%d" % j], V.tensor_copy, T.p32[:, cols(j)], bank("pa", j))
+                    else:
+                        op("v", ["%s%d" % (win, j)], ["pa%d" % j, "p32%d" % j], V.tensor_tensor, T.p32[:, cols(j)],
+                           T[win][:, cols(j)], bank("pa", j), Op.add)
+                if last:
+                    for a, b in STORES:
+                        op("y", ["p32%d" % j for j in range(a, b)], [], g.sync.dma_start, T.yg[:, CB[a]:CB[b]],
+                           T.p32[:, CB[a]:CB[b]], dma="st")
+                else:
+                    for j in ORDV:
+                        ahead(j)
+                    for j in ORDG:
+                        op("g", ["p32%d" % j], ["p16%d" % j], g.affine_select, T.p16[:, cols(j)], T.p32[:, cols(j)],
+                           [[0, CB[j + 1] - CB[j]]], Op.is_ge, 0.0, 0, 0)
+                    if VT < CB[1]:
+                        op("g", ["p320"], ["p16x"], g.affine_select, T.p16[:, VT:CB[1]], T.p32[:, VT:CB[1]],
+                           [[0, CB[1] - VT]], Op.is_ge, 0.0, 0, 0)
+                continue
+
+            def half(j):
+                op("v", [], ["%s%d" % (held(j), j), "p16%d" % j] + (["p16x"] if j == 0 else []), V.tensor_copy,
+                   T.p16[:, cols(j)], bank(held(j), j))
+
+            def full(j):
+                op("s", [], ["%s%d" % (held(j), j), "p32%d" % j], S.activation, T.p32[:, cols(j)], bank(held(j), j),
+                   Act.Copy)
+
+            spread(k + 1)
+            after(1)
+            after(0)
+            side_by_side()
+            after(3)
+            before(4)
+            after(4)
+            after(2)
+            ahead(0)
+            half(1)
+            full(0)
+            choose(k + 1)
+            half(3)
+            half(0)
+            full(1)
+            lay(t + 1, 0)
+            ahead(1)
+            full(2)
+            half(4)
+            half(2)
+            full(3)
+            full(4)
+            lay(t + 1, 1)
+
+    done = emit(g, T, ops, ext)
+    g.sync.wait_ge(T.sem.st, done["st"])
+    g.wait_ge(T.sem.ste, done["ste"])
+    g.wait_ge(T.sem.sent, RO * F * en)

@@ -2,55 +2,54 @@ from concourse.mybir import AluOpType as Op, AxisListType, ActivationFunctionTyp
 
 W, RO, F, N = 2016, 3, 2, 8
 K = W // 16
-CB = [0, 448, 832, 1344, 1728, 2016]
-NC = len(CB) - 1
-SC = (0, 2)
-HM = (0,)
-HALF = CB[2]
-SPARE = 2
+OFF, UP = 32.0, 64.0
+S0 = 2.0 ** -14
 BIG = 30000.0
-LOADS = [(0, 1), (1, 2), (2, 4), (4, 5)]
-STORES = [(4, 5), (2, 4), (0, 2)]
-VT = CB[1]
-PB2 = 4
-ORDP = (1, 2, 3, 0, 4)
-ORDL = (4, 2, 3, 0, 1)
-ORDV = (0, 2, 1, 3, 4)
-ORDG = (1, 2, 3, 4)
+A0, A1, B0 = 512, 384, 512
+U2, U1, U0A, U0B = 288, 448, 256, 0
+CS = A0 + A1
+C2, C1 = CS + U2, CS + U2 + U1
+PIECE = {"a0": (0, A0, "a0"), "a1": (A0, CS, "a1"), "b0": (0, B0, "b0"), "b1": (B0, CS, "b1"),
+         "u2": (CS, C2, "u2"), "u1": (C2, C1, "u1"), "u0": (C1, W, "u0"),
+         "u0a": (C1, C1 + U0A, "u0"), "u0b": (C1 + U0A, C1 + U0A + U0B, "u0"), "uo": (C1 + U0A + U0B, W, "u0")}
+BASE = {n: PIECE[n][0] for n in ("a0", "a1", "b0", "b1", "u2", "u1", "u0")}
+UO = W - PIECE["uo"][0]
+PHASE = ("g:u1 g:u2 g:u0a g:a0 g:a1 c:u2 c:u1 c:u0a x:b0 x:a0 c:a0 x:a1 c:a1 x:b1 v:a0 v:a1").split()
+FIRST = ("g:a0 x:a0 p:1 v:u1 g:u1 c:a0 v:u0a g:a1 x:a1 c:u1 g:u2 c:a1 g:u0a c:u2 x:b0 c:u0a x:b1 v:a0 v:a1").split()
+POST = ("u2", "b0", "u1", "b1", "u0")
+AHEAD = ("u2", "u1", "u0a")
+NP = sum(x[0] == "c" for x in PHASE)
+LOADS = [("a0", "y"), ("a1", "s"), ("u1", "y"), ("u0", "s"), ("u2", "y")]
 
 SCRATCH = {
     "gi": ("sbuf", [128, W], "int32"),
-    "p32": ("sbuf", [128, W], "float32"),
-    "p16": ("sbuf", [128, W], "float16"),
+    "x32": ("sbuf", [128, W], "float32"),
+    "x16": ("sbuf", [128, W], "float16"),
     "dl": ("sbuf", [128, W], "float16"),
     "v16": ("sbuf", [128, W], "float16"),
     "junk": ("sbuf", [128, W], "bfloat16"),
-    "h32": ("sbuf", [128, CB[1]], "float32"),
     "jj": ("sbuf", [128, 256], "float32"),
     "j16": ("sbuf", [128, 128], "float32"),
     "pint": ("sbuf", [128, 2], "int32"),
-    "col": ("sbuf", [128, 16], "float32"),
-    "acc": ("sbuf", [128, 8 * (3 * RO + 2)], "float32"),
+    "col": ("sbuf", [128, 40], "float32"),
+    "acc": ("sbuf", [128, 24], "float32"),
+    "rsc": ("sbuf", [128, 4], "float32"),
+    "rs": ("sbuf", [128, 4], "float32"),
     "ecol": ("sbuf", [128, 1], "float32"),
-    "eye": ("sbuf", [128, 128], "float16"),
-    "neye": ("sbuf", [128, 128], "float16"),
-    "ipos": ("sbuf", [128, 128], "float16"),
-    "ineg": ("sbuf", [128, 128], "float16"),
-    "keep": ("sbuf", [128, 128], "float16"),
-    "take": ("sbuf", [128, 128], "float16"),
-    "grp": ("sbuf", [128, 128], "float16"),
     "rm": ("sbuf", [128, 16], "float16"),
     "rtb": ("sbuf", [128, 16], "float16"),
+    "rk": ("sbuf", [128, 16], "float16"),
     "rr": ("sbuf", [128, 16], "float16"),
-    "cb0": ("sbuf", [128, 144], "float16"),
-    "cb": ("sbuf", [128, 144], "float16"),
-    "sel": ("sbuf", [128, 144], "float16"),
     "pe": ("psum", [128, 512], "float32"),
 }
-for _j in range(NC):
-    SCRATCH["pa%d" % _j] = ("psum", [128, 512], "float32")
-for _j in SC:
-    SCRATCH["pb%d" % _j] = ("psum", [128, 512], "float32")
+for _n in ("eye", "eyeup", "ineg", "take", "grp", "nd0", "nd1", "nd2"):
+    SCRATCH[_n] = ("sbuf", [128, 128], "float16")
+for _n in ("cb0", "cb", "sel", "selu"):
+    SCRATCH[_n] = ("sbuf", [128, 144], "float16")
+for _n in ("sv0", "sv1", "sv2"):
+    SCRATCH[_n] = ("sbuf", [128, UO], "float16")
+for _n in BASE:
+    SCRATCH[_n] = ("psum", [128, 512], "float32")
 for _t in range(RO):
     for _n in ("own", "hand", "m1_", "m2_"):
         SCRATCH["%s%d" % (_n, _t)] = ("sbuf", [128, K], "uint16")
@@ -156,11 +155,16 @@ def rank_program(g, core, T, topo):
     ext = {"m%d_%d" % (s, t): ("m%d_%d" % (s, t), arrivals(T, topo, rank, t, s))
            for t in range(RO) for s in range(1, F + 1)}
     emask, en = narrow(T, topo, core)
-    every = lambda n: ["%s%d" % (n, j) for j in range(NC)]
-    cols = lambda j: slice(CB[j], CB[j + 1])
-    bank = lambda n, j: T["%s%d" % (n, j)][:, 0:CB[j + 1] - CB[j]]
-    col = lambda k: T.col[:, k:k + 1]
-    acc = lambda k, a, b=None: T.acc[:, 8 * k + a:8 * k + (a + 1 if b is None else b)]
+    span = lambda n, a, b: ["%s:%d" % (n, j) for j in range(a // 32, (b + 31) // 32)]
+    keys = lambda n, c: span(n, PIECE[c][0], PIECE[c][1])
+    sb = lambda n, c: T[n][:, PIECE[c][0]:PIECE[c][1]]
+    bk = lambda c: PIECE[c][2]
+    ps = lambda c: T[bk(c)][:, PIECE[c][0] - BASE[bk(c)]:PIECE[c][1] - BASE[bk(c)]]
+    names = ["pf", "pm", "pg", "pg15", "tb", "thr", "mn", "kk", "nsb", "phi", "w", "fin0", "fin1", "sg0", "sg1", "sg2",
+             "psi0", "psi1", "n1", "nsk", "c0", "c1", "c2", "c3", "c4"]
+    col = lambda n: T.col[:, names.index(n):names.index(n) + 1]
+    acc = lambda a, b=None: T.acc[:, a:(a + 1 if b is None else b)]
+    ak = lambda a, b=None: ["acc%d" % j for j in range(a, a + 1 if b is None else b)]
 
     def op(q, rd, wr, fn, *args, dma=None, **kw):
         ops.append((q, lambda: fn(*args, **kw), list(rd), list(wr), dma))
@@ -171,76 +175,81 @@ def rank_program(g, core, T, topo):
         else:
             op("v", rd, wr, V.tensor_scalar, out, in0, s1, s2, o0, o1)
 
-    def mm(n, j, lhs, rhs, start=False, stop=False):
-        op("t", [lhs, "%s%d" % (rhs, j)], ["%s%d" % (n, j)], PE.matmul, bank(n, j), T[lhs][:], T[rhs][:, cols(j)],
-           start, stop)
+    def act(rd, wr, out, in_, fn=Act.Identity, **kw):
+        op("s", rd, wr, S.activation, out, in_, fn, **kw)
 
-    def count(k, j, place):
-        op("s", [], ["pa%d" % j, "junk%d" % j, "acc%d_%d" % (k, place)], S.activation, T.junk[:, cols(j)],
-           bank("pa", j), Act.Sign, bias=-0.5, scale=-1.0, accum_out=acc(k, place))
+    def mm(c, lhs, rhs, start=False, stop=False):
+        op("t", [lhs] + keys(rhs, c), [bk(c)], PE.matmul, ps(c), T[lhs][:], sb(rhs, c), start, stop)
 
-    def spot(t, h):
-        if h == 0:
-            return "pa%d" % SPARE, T["pa%d" % SPARE][:, 0:HALF // 16]
-        return "pe", T.pe[:, 16:16 + (W - HALF) // 16]
+    def ahead(c):
+        mm(c, "eyeup" if c[0] == "u" else "eye", "v16", True)
 
-    for k, (a, b) in enumerate(LOADS):
-        q, eng = (("s", S) if k == 1 else ("y", g.sync))
-        op(q, [], ["gi%d" % j for j in range(a, b)], eng.dma_start, T.gi[:, CB[a]:CB[b]], T.g0[:, CB[a]:CB[b]],
-           dma="ld%d" % k)
-    op("g", [], ["jj"], g.iota, T.jj[:], [[1, 256]], 0, 0, allow_small_or_imprecise_dtypes=True)
+    def count(c, key, out):
+        act([], [bk(c), key] + keys("junk", c), sb("junk", c), ps(c), Act.Sign, bias=-0.5, scale=-1.0, accum_out=out)
+
+    def pool_copy(c, out, in_):
+        op("g", keys(in_, c), keys(out, c), g.affine_select, sb(out, c), sb(in_, c),
+           [[0, PIECE[c][1] - PIECE[c][0]]], Op.is_ge, 0.0, 0, 0)
+
+    for k, (c, q) in enumerate(LOADS):
+        op(q, [], keys("gi", c), (S if q == "s" else g.sync).dma_start, sb("gi", c), sb("g0", c), dma="ld%d" % k)
+    loose = dict(allow_small_or_imprecise_dtypes=True)
+    op("g", [], ["jj"], g.iota, T.jj[:], [[1, 256]], 0, 0, **loose)
     op("g", [], ["pint0"], g.iota, T.pint[:, 0:1], [[0, 1]], 0, 1)
-    op("g", [], ["j16"], g.iota, T.j16[:], [[16, 8], [0, 16]], 0, 0, allow_small_or_imprecise_dtypes=True)
-    PF, PM, PG, PG15, TB, THR, NPART, MN = range(8)
+    op("g", [], ["j16"], g.iota, T.j16[:], [[16, 8], [0, 16]], 0, 0, **loose)
+    op("g", [], ak(0, 24), g.iota, T.acc[:], [[-1, 24]], NP, 0, **loose)
     J = T.jj[:, 0:128]
-    op("v", ["jj"], ["va"], V.tensor_copy, T.v16[:, 0:256], T.jj[:])
-    ts(["jj"], ["vb"], T.v16[:, 256:512], T.jj[:], 256.0, None, Op.add)
-    op("v", ["pint0"], ["pf"], V.tensor_copy, col(PF), T.pint[:, 0:1])
+    ts(["jj"], span("v16", 0, 256), T.v16[:, 0:256], T.jj[:], OFF, None, Op.add)
+    act(["jj"], span("v16", 256, 512), T.v16[:, 256:512], T.jj[:], bias=256.0 + OFF)
+    op("v", ["pint0"], ["pf"], V.tensor_copy, col("pf"), T.pint[:, 0:1])
     ts(["pint0"], ["pint1"], T.pint[:, 1:2], T.pint[:, 0:1], 15, None, Op.bitwise_and)
-    ts(["va", "vb"], ["v160", "v161"], T.v16[:, 512:1024], T.v16[:, 0:512], 512.0, None, Op.add)
-    ts(["jj", "pf"], ["eye"], T.eye[:], J, col(PF), None, Op.is_equal)
-    ts(["jj", "pf"], ["neye"], T.neye[:], J, col(PF), -1.0, Op.is_equal, Op.mult)
-    op("v", ["pint1"], ["pm"], V.tensor_copy, col(PM), T.pint[:, 1:2])
-    ts(["v161"], ["v162", "v163", "v164"], T.v16[:, 1024:W], T.v16[:, 0:W - 1024], 1024.0, None, Op.add)
-    ts(["pf", "pm"], ["pg"], col(PG), col(PF), col(PM), None, Op.subtract)
-    ts(["pf", "pm"], ["pg15"], col(PG15), col(PF), col(PM), 15.0, Op.subtract, Op.add)
-    ts(["pm"], ["tb"], col(TB), col(PM), 0.125, None, Op.mult)
-    ts(["jj", "pm"], ["rm"], T.rm[:], T.jj[:, 0:16], col(PM), None, Op.is_equal)
+    ts(["jj", "pf"], ["eye"], T.eye[:], J, col("pf"), None, Op.is_equal)
+    ts(span("v16", 0, 512), span("v16", 512, 1024), T.v16[:, 512:1024], T.v16[:, 0:512], 512.0, None, Op.add)
+    op("v", ["pint1"], ["pm"], V.tensor_copy, col("pm"), T.pint[:, 1:2])
+    ts(span("v16", 0, 992), span("v16", 1024, W), T.v16[:, 1024:W], T.v16[:, 0:W - 1024], 1024.0, None, Op.add)
+    act(["eye"], ["nd0"], T.nd0[:], T.eye[:], scale=-1 / S0)
+    act(["eye"], ["eyeup"], T.eyeup[:], T.eye[:], scale=UP)
+    act(["eye"], ["ineg"], T.ineg[:], T.eye[:], scale=BIG, bias=-BIG)
+    act(["pf", "pm"], ["pg"], col("pg"), col("pm"), scale=-1.0, bias=col("pf"))
+    act(["pm"], ["tb"], col("tb"), col("pm"), scale=0.125)
+    act(["pg"], ["pg15"], col("pg15"), col("pg"), bias=15.0)
+    act(keys("v16", "uo"), ["sv0"], T.sv0[:], sb("v16", "uo"), scale=S0)
     late = [
-        lambda: ts(["j16", "pg"], ["grp"], T.grp[:], T.j16[:], col(PG), None, Op.is_equal),
-        lambda: ts(["jj", "pg15"], ["cb0"], T.cb0[:], T.jj[:, 0:144], col(PG15), BIG, Op.not_equal, Op.mult),
-        lambda: ts(["jj", "pm", "tb"], ["rtb"], T.rtb[:], T.jj[:, 0:16], col(PM), col(TB), Op.is_equal, Op.mult),
-        lambda: ts(["cb0", "tb"], ["cb"], T.cb[:], T.cb0[:], col(TB), None, Op.add),
-        lambda: ts(["jj", "pf"], ["ipos"], T.ipos[:], J, col(PF), BIG, Op.not_equal, Op.mult),
-        lambda: ts(["jj", "pf"], ["ineg"], T.ineg[:], J, col(PF), -BIG, Op.not_equal, Op.mult),
+        [lambda: ts(["jj", "pm"], ["rm"], T.rm[:], T.jj[:, 0:16], col("pm"), None, Op.is_equal),
+         lambda: ts(["j16", "pg"], ["grp"], T.grp[:], T.j16[:], col("pg"), None, Op.is_equal)],
+        [lambda: ts(["jj", "pg15"], ["cb0"], T.cb0[:], T.jj[:, 0:144], col("pg15"), BIG, Op.not_equal, Op.mult),
+         lambda: ts(["jj", "pm", "tb"], ["rtb"], T.rtb[:], T.jj[:, 0:16], col("pm"), col("tb"), Op.is_equal, Op.mult)],
+        [lambda: ts(["cb0", "tb"], ["cb"], T.cb[:], T.cb0[:], col("tb"), None, Op.add)],
+        [], [],
     ]
 
     def ties():
         op("t", ["grp", "rtb"], ["pe"], PE.matmul, T.pe[:, 0:16], T.grp[:], T.rtb[:], True, False)
 
-    def spread(k):
-        ts(["rm", "acc%d_4" % k], ["rr"], T.rr[:], T.rm[:], acc(k, 4), None, Op.mult)
+    def side_by_side(n, stop):
+        op("t", ["grp", n], ["pe"], PE.matmul, T.pe[:, 0:16], T.grp[:], T[n][:], False, stop)
 
-    def side_by_side():
-        op("t", ["grp", "rr"], ["pe"], PE.matmul, T.pe[:, 0:16], T.grp[:], T.rr[:], False, True)
+    def least():
+        op("v", [], ["pe", "mn"], V.tensor_reduce, col("mn"), T.pe[:, 0:16], X, Op.min)
 
-    def choose(k):
-        op("v", [], ["pe", "mn"], V.tensor_reduce, col(MN), T.pe[:, 0:16], X, Op.min)
-        ts(["cb", "mn", "acc%d_4" % k], ["sel"], T.sel[:], T.cb[:], acc(k, 4), col(MN), Op.add, Op.is_le)
+    def choose(key, own):
+        ts(["cb", "mn", key], ["sel"], T.sel[:], T.cb[:], own, col("mn"), Op.add, Op.is_le)
 
-    def lay(t, h):
-        lo, hi = (0, HALF) if h == 0 else (HALF, W)
-        src = ["p16%d" % j for j in range(NC) if lo <= CB[j] < hi]
-        key, out = spot(t, h)
+    def spot(h):
+        if h == 0:
+            return 0, CS, "pe", T.pe[:, 16:16 + CS // 16]
+        return CS, W, "b0", T.b0[:, 0:(W - CS) // 16]
+
+    def lay(h, sel):
+        lo, hi, key, out = spot(h)
         for a in range(16):
-            op("t", ["sel"] + src, [key], PE.matmul, out, T.sel[:, 15 - a:143 - a], T.p16[:, lo + a:hi:16],
-               a == 0, a == 15)
+            op("t", [sel] + span("x16", lo, hi), [key], PE.matmul, out, T[sel][:, 15 - a:143 - a],
+               T.x16[:, lo + a:hi:16], a == 0, a == 15)
 
-    def publish(t, h):
+    def publish(t, h, scale):
         own = T["own%d" % t]
-        lo, hi = (0, HALF // 16) if h == 0 else (HALF // 16, K)
-        key, src = spot(t, h)
-        op("v", [], [key, "own%d_%d" % (t, h)], V.tensor_copy, own[:, lo:hi], src)
+        lo, hi, key, src = spot(h)
+        ts([], [key, "own%d_%d" % (t, h)], own[:, lo // 16:hi // 16], src, scale, -OFF, Op.mult, Op.add)
         for s in (range(1, F + 1) if h == 1 else []):
             dst, via = route(T, topo, rank, t, s)
             to, name = (dst, "m%d_%d" % (s, t)) if via is None else (via, "hand%d" % t)
@@ -248,168 +257,199 @@ def rank_program(g, core, T, topo):
             op("g", ["own%d_0" % t, "own%d_1" % t], [], g.remote_dma, T[name][:], own[:], T.sem[name], T.sem.sent,
                pid, rid, emask, dma="sent")
 
-    def ahead(j):
-        mm("pa", j, "eye", "v16", True)
-
-    def minus_p(j):
-        if j not in HM:
-            mm("pa", j, "neye", "p16")
-
-    for j in range(NC):
-        ahead(j)
-    for j in range(NC):
-        op("v", ["gi%d" % j], ["p16%d" % j], V.tensor_copy, T.p16[:, cols(j)], T.gi[:, cols(j)])
-        mm("pa", j, "neye", "p16", False, True)
-        count(0, j, j)
-        if j < 2:
-            for f in late[3 * j:3 * j + 3]:
-                f()
+    for c, q in LOADS:
+        mm(c, "eye", "v16", True)
+    for j, (c, q) in enumerate(LOADS):
+        ts(keys("gi", c), keys("x16", c), sb("x16", c), sb("gi", c), OFF, S0, Op.add, Op.mult)
+        mm(c, "nd0", "x16", False, True)
+        count(c, "c%d" % j, col("c%d" % j))
+        if j < 3:
+            pool_copy(c, "x32", "x16")
+        for f in late[j]:
+            f()
         if j == 2:
             ties()
-            ahead(0)
-        if j == 4:
-            ahead(1)
-            minus_p(1)
-    op("v", ["acc0_%d" % j for j in range(NC)], ["acc1_4"], V.tensor_reduce, acc(1, 4), acc(0, 0, NC), X, Op.add,
-       negate=True)
-    spread(1)
-    side_by_side()
-    choose(1)
-    lay(0, 0)
-    lay(0, 1)
+            ahead("a0")
+        if j == 3:
+            ahead("a1")
+    c0 = names.index("c0")
+    op("v", ["c%d" % j for j in range(5)], ak(0), V.tensor_reduce, acc(0), T.col[:, c0:c0 + 5], X, Op.add, negate=True)
+    ts(["rm"] + ak(0), ["rr"], T.rr[:], T.rm[:], acc(0), None, Op.mult)
+    side_by_side("rr", True)
+    for c, q in LOADS[3:]:
+        act(keys("x16", c), keys("x32", c), sb("x32", c), sb("x16", c), Act.Copy)
+    least()
+    ahead("u2")
+    choose("acc0", acc(0))
+    for j, x in enumerate((1.0, (UP - 1) / (2 * UP), (UP + 1) / (2 * UP))):
+        op("v", [], ["rsc%d" % j], V.memset, T.rsc[:, j:j + 1], x)
+    lay(0, "sel")
+    lay(1, "sel")
+    publish(0, 0, 1 / S0)
+
+    def gain(k):
+        fin = "fin%d" % (k % 2)
+        ts(["thr", fin], ak(k), acc(k), col("thr"), col(fin), 1.0, Op.subtract, Op.min)
 
     for t in range(RO):
         for s in range(F + 1):
             k = 3 * t + s + 1
             last = t == RO - 1 and s == F
             turn = s == F and not last
-            win = "gi" if k == 1 else "p32"
             lst = "own%d" % t if s == 0 else "m%d_%d" % (s, t)
+            nd, sv = "nd%d" % s, "sv%d" % s
+            fin, sg = "fin%d" % (k % 2), "sg%d" % s
+            place = [k + 1]
 
-            def picked(a, b):
-                return T[win][:, 0:W].indirect(T[lst][:, a // 16:b // 16])
+            def picked(c):
+                a, b = PIECE[c][0:2]
+                rd = span("x32", 0, W) + [lst if s else "%s_%d" % (lst, int(a >= CS))]
+                return rd, T.x32[:, 0:W].indirect(T[lst][:, a // 16:b // 16])
 
-            def name(a):
-                return lst if s else "%s_%d" % (lst, int(a >= HALF))
-
-            def gather(j, a, b):
-                if j in HM:
-                    op("v", every(win) + [name(a)], ["dl%d" % j], V.tensor_copy, T.dl[:, a:b], picked(a, b))
+            def gather(c):
+                rd, src = picked(c)
+                if c == "u1":
+                    act(rd, keys("dl", c), sb("dl", c), src, Act.Copy, scale=UP)
+                elif c[0] == "u":
+                    ts(rd, keys("dl", c), sb("dl", c), src, UP, None, Op.mult)
                 else:
-                    op("v", every(win) + [name(a), "p16%d" % j], ["dl%d" % j], V.tensor_tensor, T.dl[:, a:b],
-                       picked(a, b), T.p16[:, a:b], Op.subtract)
+                    op("v", rd + keys("x16", c), keys("dl", c), V.tensor_tensor, sb("dl", c), src, sb("x16", c),
+                       Op.subtract)
 
-            def held(j):
-                return "pb" if j in SC else "pa"
-
-            def before(j):
-                if j not in HM:
-                    mm(held(j), j, "eye", "p16", True)
-
-            def after(j):
-                if j in HM:
-                    op("t", ["keep", "p16%d" % j, "p16x"], ["%s%d" % (held(j), j)], PE.matmul, bank(held(j), j),
-                       T.keep[:], T.p16[:, cols(j)], True, False)
-                mm(held(j), j, "take", "dl", not (j in HM or j in SC or turn), True)
-
-            order = [0, 1, 2, 3, 4] if k == 1 else [1, 0, 2, 3, 4]
-            if s == 0:
-                publish(t, 0)
-            if k > 1:
-                op("s", every(win) + [name(0)], ["h32"], S.activation, T.h32[:], picked(0, CB[1]), Act.Copy)
-            for j in order:
-                if s == 0 and j >= 2:
-                    ahead(j)
-                if not (k == 1 and j == 1):
-                    minus_p(j)
-                if j == order[0] and s == 0:
-                    mid = (CB[j] + CB[j + 1]) // 64 * 32
-                    gather(j, CB[j], mid)
-                    publish(t, 1)
-                    gather(j, mid, CB[j + 1])
-                elif j == 0:
-                    op("v", ["h32"], ["dl0"], V.tensor_copy, T.dl[:, cols(0)], T.h32[:])
+            def tally(c):
+                mm(c, nd, "dl", False, True)
+                if place[0] < k + NP:
+                    count(c, ak(place[0])[0], acc(place[0]))
                 else:
-                    gather(j, CB[j], CB[j + 1])
-                mm("pa", j, "neye", "dl", False, True)
-                count(k, j, j if j < NC - 1 else 5)
-                if j == PB2:
-                    before(2)
-                if turn and j == 3:
-                    before(1)
-                    ties()
-                if turn and j == 4:
-                    before(3)
+                    count(c, fin, col(fin))
+                place[0] += 1
+
+            for what, c in (x.split(":") for x in (PHASE if s else FIRST)):
+                if what == "g":
+                    gather(c)
+                elif what == "c":
+                    tally(c)
+                elif what == "p":
+                    publish(t, 1, 1.0 if t else 1 / S0)
+                elif what == "x" and c[0] == "a":
+                    mm(c, nd, "x16")
+                elif what == "x":
+                    mm(c, "eye", "x16", True)
+                elif not (last and c[0] == "a"):
+                    ahead(c)
+            rd, src = picked("uo")
+            op("v", rd + [sv], keys("junk", "uo"), V.tensor_tensor, sb("junk", "uo"), src, T[sv][:], Op.is_gt)
             if s:
-                op("v", ["p320"], ["p160"], V.tensor_copy, T.p16[:, 0:VT], T.p32[:, 0:VT])
-            a4 = ["acc%d_%d" % (k, j) for j in range(4)]
-            ns, fin = "acc%d_4" % k, "acc%d_5" % k
-            op("v", a4 + [ns], ["thr"], V.tensor_reduce, col(THR), acc(k, 0, 5), X, Op.add, negate=True)
-            op("v", a4, ["npart"], V.tensor_reduce, col(NPART), acc(k, 0, 4), X, Op.add, negate=True)
-            ts(["ineg", fin, "thr"], ["take"], T.take[:], T.ineg[:], acc(k, 5), col(THR), Op.add, Op.is_gt)
-            ts(["ipos", fin, "thr"], ["keep"], T.keep[:], T.ipos[:], acc(k, 5), col(THR), Op.add, Op.is_le)
-            ts(["npart", fin, ns], ["acc%d_4" % (k + 1)], acc(k + 1, 4), col(NPART), acc(k, 5), acc(k, 4),
-               Op.subtract, Op.min)
+                gain(k - 1)
+            op("v", keys("junk", "uo"), ["n1"], V.tensor_reduce, col("n1"), sb("junk", "uo"), X, Op.add)
+            if last:
+                ts(["psi0"], ["psi0"], col("psi0"), col("psi0"), 1 / S0, None, Op.mult)
+            if s == F:
+                op("v", ak(0, k), ["nsb"], V.tensor_reduce, col("nsb"), acc(0, k), X, Op.add)
+            ts(["n1"], ak(k), acc(k), col("n1"), 2.0, -float(UO), Op.mult, Op.add)
+            if s == F:
+                ts(["rsc0", "rsc1", "rsc2", "psi0", "psi1"], ["rs"], T.rs[:, 0:3], T.rsc[:, 0:3], col("psi0"),
+                   col("psi1"), Op.mult, Op.mult)
+            if turn:
+                ts(["rm", "nsb"], ["rk"], T.rk[:], T.rm[:], col("nsb"), None, Op.mult)
+                ts(["nsb"], ["nsk"], col("nsk"), col("nsb"), -16.0, None, Op.add)
+                ties()
+                side_by_side("rk", False)
+            op("v", ak(0, k + NP + 1), ["thr"], V.tensor_reduce, col("thr"), acc(0, k + NP + 1), X, Op.add, negate=True)
 
-            if not turn:
-                if last:
-                    ts(["acc%d_4" % (k + 1)], ["ecol"], T.ecol[:], acc(k + 1, 4), -0.5, W / 2, Op.mult, Op.add)
-                    op("g", ["ecol"], [], g.dma_start, T.ye[:], T.ecol[:], dma="ste", allow_slow_non_contiguous=True)
-                for j in (ORDL if last else ORDP):
-                    after(j)
-                    if j in SC:
-                        op("s", [], ["pb%d" % j, "p32%d" % j], S.activation, T.p32[:, cols(j)], bank("pb", j), Act.Copy)
-                    elif j in HM:
-                        op("v", [], ["pa%d" % j, "p32%d" % j], V.tensor_copy, T.p32[:, cols(j)], bank("pa", j))
+            def take():
+                ts(["ineg", fin, "thr"], ["take"], T.take[:], T.ineg[:], col(fin), col("thr"), Op.add, Op.is_gt)
+
+            def larger(c, out):
+                op("v", keys("x32", c), [bk(c)] + keys(out, c), V.tensor_tensor, sb(out, c), sb("x32", c), ps(c), Op.max)
+
+            def after(c):
+                mm(c, "take", "dl", c[0] == "u", True)
+
+            act([fin, "thr"], [sg], col(sg), col(fin), Act.Sign, bias=col("thr"), scale=-1.0)
+            if s < F:
+                psi = "psi%d" % s
+                act([sg], ["phi"], col("phi"), col(sg), bias=(UP + 1) / 2, scale=-(UP - 1) / 2)
+                act([sg], [psi], col(psi), col(sg), bias=(UP + 1) / (2 * UP), scale=(UP - 1) / (2 * UP))
+                take()
+                gather("uo")
+                for c in POST:
+                    after(c)
+                    if c[0] == "u":
+                        larger(c, "x32")
                     else:
-                        op("v", ["%s%d" % (win, j)], ["pa%d" % j, "p32%d" % j], V.tensor_tensor, T.p32[:, cols(j)],
-                           T[win][:, cols(j)], bank("pa", j), Op.add)
-                if last:
-                    for a, b in STORES:
-                        op("y", ["p32%d" % j for j in range(a, b)], [], g.sync.dma_start, T.yg[:, CB[a]:CB[b]],
-                           T.p32[:, CB[a]:CB[b]], dma="st")
-                else:
-                    for j in ORDV:
-                        ahead(j)
-                    for j in ORDG:
-                        op("g", ["p32%d" % j], ["p16%d" % j], g.affine_select, T.p16[:, cols(j)], T.p32[:, cols(j)],
-                           [[0, CB[j + 1] - CB[j]]], Op.is_ge, 0.0, 0, 0)
-                    if VT < CB[1]:
-                        op("g", ["p320"], ["p16x"], g.affine_select, T.p16[:, VT:CB[1]], T.p32[:, VT:CB[1]],
-                           [[0, CB[1] - VT]], Op.is_ge, 0.0, 0, 0)
+                        act(["phi"], [c] + keys("x32", c), sb("x32", c), ps(c), Act.Copy, scale=col("phi"))
+                        pool_copy(c, "x16", "x32")
+                    if c == POST[0]:
+                        ts([nd, psi], ["nd%d" % (s + 1)], T["nd%d" % (s + 1)][:], T[nd][:], col(psi), None, Op.mult)
+                act([sv, "phi"], ["sv%d" % (s + 1)], T["sv%d" % (s + 1)][:], T[sv][:], Act.Copy, scale=col("phi"))
+                for c in AHEAD:
+                    ahead(c)
                 continue
 
-            def half(j):
-                op("v", [], ["%s%d" % (held(j), j), "p16%d" % j] + (["p16x"] if j == 0 else []), V.tensor_copy,
-                   T.p16[:, cols(j)], bank(held(j), j))
+            act([sg, "rs"], ["w"], col("w"), col(sg), bias=T.rs[:, 2:3], scale=T.rs[:, 1:2])
+            if last:
+                take()
+                gather("uo")
 
-            def full(j):
-                op("s", [], ["%s%d" % (held(j), j), "p32%d" % j], S.activation, T.p32[:, cols(j)], bank(held(j), j),
-                   Act.Copy)
+                def store(c):
+                    op("y", keys("x32", c), [], g.sync.dma_start, sb("yg", c), sb("x32", c), dma="st")
 
-            spread(k + 1)
-            after(1)
-            after(0)
-            side_by_side()
-            after(3)
-            before(4)
-            after(4)
-            after(2)
-            ahead(0)
-            half(1)
-            full(0)
-            choose(k + 1)
-            half(3)
-            half(0)
-            full(1)
-            lay(t + 1, 0)
-            ahead(1)
-            full(2)
-            half(4)
-            half(2)
-            full(3)
-            full(4)
-            lay(t + 1, 1)
+                for c in ("b1", "b0", "u2", "u1", "u0"):
+                    after(c)
+                ts(["rs"], ["b1"] + keys("x32", "b1"), sb("x32", "b1"), ps("b1"), T.rs[:, 0:1], -OFF, Op.mult, Op.add)
+                store("b1")
+                act(["rs"], ["b0"] + keys("x32", "b0"), sb("x32", "b0"), ps("b0"), bias=-OFF, scale=T.rs[:, 0:1])
+                store("b0")
+                gain(k)
+                for c in ("u2", "u1", "u0"):
+                    larger(c, "x16")
+                    act(["w"] + keys("x16", c), keys("x32", c), sb("x32", c), sb("x16", c), bias=-OFF, scale=col("w"))
+                    store(c)
+                    if c == "u2":
+                        ts(ak(k) + ["nsb"], ["kk"], col("kk"), acc(k), col("nsb"), -float(W + k), Op.add, Op.add)
+                    if c == "u1":
+                        ts(["kk"], ["ecol"], T.ecol[:], col("kk"), -0.5, None, Op.mult)
+                        op("g", ["ecol"], [], g.dma_start, T.ye[:], T.ecol[:], dma="ste", allow_slow_non_contiguous=True)
+                continue
+
+            def plain(c, out):
+                act(["rs"], [c] + keys(out, c), sb(out, c), ps(c), Act.Copy, scale=T.rs[:, 0:1])
+
+            def level(q, c):
+                if q == "s":
+                    act(["w"] + keys("x16", c), keys("x32", c), sb("x32", c), sb("x16", c), Act.Copy, scale=col("w"))
+                else:
+                    ts(["w"] + keys("x16", c), keys("x32", c), sb("x32", c), sb("x16", c), col("w"), None, Op.mult)
+
+            take()
+            gain(k)
+            gather("uo")
+            ts(["rm"] + ak(k), ["rr"], T.rr[:], T.rm[:], acc(k), -1.0, Op.mult, Op.add)
+            act(ak(k) + ["nsk"], ["kk"], col("kk"), acc(k), bias=col("nsk"))
+            after("b0")
+            after("u2")
+            side_by_side("rr", True)
+            after("b1")
+            after("u1")
+            after("u0")
+            plain("b0", "x16")
+            pool_copy("b0", "x32", "x16")
+            least()
+            larger("u2", "x16")
+            plain("b1", "x16")
+            choose("kk", col("kk"))
+            larger("u1", "x16")
+            larger("u0", "x16")
+            ts(["sel", "w"], ["selu"], T.selu[:], T.sel[:], col("w"), 1 / S0, Op.mult, Op.mult)
+            ahead("u2")
+            lay(0, "sel")
+            plain("b1", "x32")
+            level("s", "u2")
+            level("s", "u1")
+            lay(1, "selu")
+            level("v", "u0")
+            publish(t + 1, 0, 1 / S0)
 
     done = emit(g, T, ops, ext)
     g.sync.wait_ge(T.sem.st, done["st"])

@@ -5,21 +5,26 @@ K = W // 16
 OFF, UP = 32.0, 64.0
 S0 = 2.0 ** -14
 BIG = 30000.0
-A0, A1, B0 = 512, 384, 512
-U2, U1, U0A, U0B = 288, 448, 256, 0
+A0, A1, B0 = 448, 352, 448
+U2, U1, U0A, U0B = 256, 480, 288, 0
+U1A = 160
 CS = A0 + A1
 C2, C1 = CS + U2, CS + U2 + U1
 PIECE = {"a0": (0, A0, "a0"), "a1": (A0, CS, "a1"), "b0": (0, B0, "b0"), "b1": (B0, CS, "b1"),
          "u2": (CS, C2, "u2"), "u1": (C2, C1, "u1"), "u0": (C1, W, "u0"),
-         "u0a": (C1, C1 + U0A, "u0"), "u0b": (C1 + U0A, C1 + U0A + U0B, "u0"), "uo": (C1 + U0A + U0B, W, "u0")}
+         "u0a": (C1, C1 + U0A, "u0"), "u0b": (C1 + U0A, C1 + U0A + U0B, "u0"), "uo": (C1 + U0A + U0B, W, "u0"),
+         "u1a": (C2, C2 + U1A, "u1"), "u1b": (C2 + U1A, C1, "u1")}
 BASE = {n: PIECE[n][0] for n in ("a0", "a1", "b0", "b1", "u2", "u1", "u0")}
 UO = W - PIECE["uo"][0]
-PHASE = ("g:u1 g:u2 g:u0a g:a0 g:a1 c:u2 c:u1 c:u0a x:b0 x:a0 c:a0 x:a1 c:a1 x:b1 v:a0 v:a1").split()
-FIRST = ("g:a0 x:a0 p:1 v:u1 g:u1 c:a0 v:u0a g:a1 x:a1 c:u1 g:u2 c:a1 g:u0a c:u2 x:b0 c:u0a x:b1 v:a0 v:a1").split()
-POST = ("u2", "b0", "u1", "b1", "u0")
-AHEAD = ("u2", "u1", "u0a")
+PHASE = ("g:u1 g:u2 g:u0a g:a0 g:a1 c:u2 c:u1 c:u0a x:b0 x:a0 c:a0 x:a1 c:a1 x:b1 v:a0").split()
+FIRST = ("g:a0 g:a1 p:1 g:u1a g:u1b g:u0a g:u2 x:a0 c:a1 c:a0 v:u1 c:u1 v:u0a c:u0a x:b0 c:u2 v:a0").split()
+POST = ("t:u1 t:b0 t:u0 t:u2 t:b1 n:psi n:sv w:u1 w:b0 w:u0 w:u2 w:b1 n:nd v:u1 v:a1 v:u0a v:u2").split()
+TURN = ("e:rr g:uo e:kk v:a1 t:b0 e:side t:u2 t:b1 t:u1 t:u0 e:min h:u2 h:b0 h:b1 e:w G:b0 e:sel h:u1 S:b1 S:u1 S:u2 h:u0 v:u2 e:lay0 e:selu e:lay1 V:u0 e:own0").split()
 NP = sum(x[0] == "c" for x in PHASE)
-LOADS = [("a0", "y"), ("a1", "s"), ("u1", "y"), ("u0", "s"), ("u2", "y")]
+LOADS = [("a1", "y"), ("u1", "s"), ("a0", "y"), ("u0a", "s"), ("u2", "y"), ("uo", "s")]
+START = ("a1", "u1", "a0", "u0a", "u2")
+POOLED = 3
+LIST = UO + NP - 1
 
 SCRATCH = {
     "gi": ("sbuf", [128, W], "int32"),
@@ -31,18 +36,17 @@ SCRATCH = {
     "jj": ("sbuf", [128, 256], "float32"),
     "j16": ("sbuf", [128, 128], "float32"),
     "pint": ("sbuf", [128, 2], "int32"),
-    "col": ("sbuf", [128, 40], "float32"),
-    "acc": ("sbuf", [128, 24], "float32"),
-    "rsc": ("sbuf", [128, 4], "float32"),
-    "rs": ("sbuf", [128, 4], "float32"),
-    "ecol": ("sbuf", [128, 1], "float32"),
+    "col": ("sbuf", [128, 32], "float32"),
+    "acc": ("sbuf", [128, LIST + 16], "float32"),
+    "ecol": ("sbuf", [128, 1], "float16"),
+    "erow": ("sbuf", [128, 128], "float32"),
     "rm": ("sbuf", [128, 16], "float16"),
     "rtb": ("sbuf", [128, 16], "float16"),
     "rk": ("sbuf", [128, 16], "float16"),
     "rr": ("sbuf", [128, 16], "float16"),
     "pe": ("psum", [128, 512], "float32"),
 }
-for _n in ("eye", "eyeup", "ineg", "take", "grp", "nd0", "nd1", "nd2"):
+for _n in ("eye", "eyeup", "ipos", "ineg", "take", "keep", "grp", "nd0", "nd1", "nd2"):
     SCRATCH[_n] = ("sbuf", [128, 128], "float16")
 for _n in ("cb0", "cb", "sel", "selu"):
     SCRATCH[_n] = ("sbuf", [128, 144], "float16")
@@ -54,7 +58,7 @@ for _t in range(RO):
     for _n in ("own", "hand", "m1_", "m2_"):
         SCRATCH["%s%d" % (_n, _t)] = ("sbuf", [128, K], "uint16")
 
-SEMAPHORES = (["cv", "cs", "ct", "cg", "st", "ste", "sent"] + ["ld%d" % k for k in range(len(LOADS))]
+SEMAPHORES = (["cv", "cs", "ct", "cg", "st", "sent"] + ["ld%d" % k for k in range(len(LOADS))]
               + ["%s%d" % (n, t) for t in range(RO) for n in ("hand", "m1_", "m2_")])
 
 
@@ -68,15 +72,16 @@ def route(T, topo, r, t, s):
     return dst, (near or able)[0]
 
 
+def narrow(T, topo, core, half=False):
+    far = [c for c in T.cores if c not in topo.cores_of(core) and topo.may_write(core, c)]
+    eng = topo.engines(core, far[0])
+    return sum(1 << e for e in eng), len(eng)
+
+
 def arrivals(T, topo, r, t, s):
     q = (r + 1 + (F * t + s - 1) % (N - 1)) % N
     dst, via = route(T, topo, q, t, s)
-    return len(topo.engines(T.cores[q] if via is None else via, dst))
-
-
-def narrow(T, topo, core):
-    far = [c for c in T.cores if c != core and topo.may_write(core, c)]
-    return topo.mask(core, far[0]), len(topo.engines(core, far[0]))
+    return narrow(T, topo, T.cores[q])[1] if via is None else narrow(T, topo, via, t == 0)[1]
 
 
 def relay_program(g, core, T, topo):
@@ -87,11 +92,12 @@ def relay_program(g, core, T, topo):
                 dst, via = route(T, topo, r, t, s)
                 if via != core:
                     continue
-                g.wait_ge(T.sem["hand%d" % t], narrow(T, topo, T.cores[r])[1])
+                mask, n = narrow(T, topo, core, t == 0)
+                g.wait_ge(T.sem["hand%d" % t], narrow(T, topo, T.cores[r], t == 0)[1])
                 rid, pid = topo.addr(dst, core)
                 g.remote_dma(T["m%d_%d" % (s, t)][:], T["hand%d" % t][:], T.sem["m%d_%d" % (s, t)], T.sem.sent,
-                             pid, rid, topo.mask(core, dst))
-                sent += len(topo.engines(core, dst))
+                             pid, rid, mask)
+                sent += n
     if sent:
         g.wait_ge(T.sem.sent, sent)
 
@@ -154,14 +160,14 @@ def rank_program(g, core, T, topo):
     ops = []
     ext = {"m%d_%d" % (s, t): ("m%d_%d" % (s, t), arrivals(T, topo, rank, t, s))
            for t in range(RO) for s in range(1, F + 1)}
-    emask, en = narrow(T, topo, core)
+    sent = [0]
     span = lambda n, a, b: ["%s:%d" % (n, j) for j in range(a // 32, (b + 31) // 32)]
     keys = lambda n, c: span(n, PIECE[c][0], PIECE[c][1])
     sb = lambda n, c: T[n][:, PIECE[c][0]:PIECE[c][1]]
     bk = lambda c: PIECE[c][2]
     ps = lambda c: T[bk(c)][:, PIECE[c][0] - BASE[bk(c)]:PIECE[c][1] - BASE[bk(c)]]
-    names = ["pf", "pm", "pg", "pg15", "tb", "thr", "mn", "kk", "nsb", "phi", "w", "fin0", "fin1", "sg0", "sg1", "sg2",
-             "psi0", "psi1", "n1", "nsk", "c0", "c1", "c2", "c3", "c4"]
+    names = ["pf", "pm", "pg", "pg15", "tb", "thr", "mn", "kk", "nsb", "phi", "w", "wu", "rho", "fin", "tk",
+             "psi0", "psi1", "psi2", "c0", "c1", "c2", "c3", "c4", "c5"]
     col = lambda n: T.col[:, names.index(n):names.index(n) + 1]
     acc = lambda a, b=None: T.acc[:, a:(a + 1 if b is None else b)]
     ak = lambda a, b=None: ["acc%d" % j for j in range(a, a + 1 if b is None else b)]
@@ -185,11 +191,14 @@ def rank_program(g, core, T, topo):
         mm(c, "eyeup" if c[0] == "u" else "eye", "v16", True)
 
     def count(c, key, out):
-        act([], [bk(c), key] + keys("junk", c), sb("junk", c), ps(c), Act.Sign, bias=-0.5, scale=-1.0, accum_out=out)
+        act([], [bk(c), key] + keys("junk", c), sb("junk", c), ps(c), Act.Sign, bias=0.5, accum_out=out)
 
     def pool_copy(c, out, in_):
         op("g", keys(in_, c), keys(out, c), g.affine_select, sb(out, c), sb(in_, c),
            [[0, PIECE[c][1] - PIECE[c][0]]], Op.is_ge, 0.0, 0, 0)
+
+    def total(out, rd, src, negate):
+        op("v", rd, [out], V.tensor_reduce, col(out), src, X, Op.add, negate=negate)
 
     for k, (c, q) in enumerate(LOADS):
         op(q, [], keys("gi", c), (S if q == "s" else g.sync).dma_start, sb("gi", c), sb("g0", c), dma="ld%d" % k)
@@ -197,30 +206,26 @@ def rank_program(g, core, T, topo):
     op("g", [], ["jj"], g.iota, T.jj[:], [[1, 256]], 0, 0, **loose)
     op("g", [], ["pint0"], g.iota, T.pint[:, 0:1], [[0, 1]], 0, 1)
     op("g", [], ["j16"], g.iota, T.j16[:], [[16, 8], [0, 16]], 0, 0, **loose)
-    op("g", [], ak(0, 24), g.iota, T.acc[:], [[-1, 24]], NP, 0, **loose)
     J = T.jj[:, 0:128]
     ts(["jj"], span("v16", 0, 256), T.v16[:, 0:256], T.jj[:], OFF, None, Op.add)
     act(["jj"], span("v16", 256, 512), T.v16[:, 256:512], T.jj[:], bias=256.0 + OFF)
     op("v", ["pint0"], ["pf"], V.tensor_copy, col("pf"), T.pint[:, 0:1])
     ts(["pint0"], ["pint1"], T.pint[:, 1:2], T.pint[:, 0:1], 15, None, Op.bitwise_and)
-    ts(["jj", "pf"], ["eye"], T.eye[:], J, col("pf"), None, Op.is_equal)
     ts(span("v16", 0, 512), span("v16", 512, 1024), T.v16[:, 512:1024], T.v16[:, 0:512], 512.0, None, Op.add)
+    act(span("v16", 0, 480), span("v16", 1536, W), T.v16[:, 1536:W], T.v16[:, 0:W - 1536], bias=1536.0)
+    ts(["jj", "pf"], ["eye"], T.eye[:], J, col("pf"), None, Op.is_equal)
     op("v", ["pint1"], ["pm"], V.tensor_copy, col("pm"), T.pint[:, 1:2])
-    ts(span("v16", 0, 992), span("v16", 1024, W), T.v16[:, 1024:W], T.v16[:, 0:W - 1024], 1024.0, None, Op.add)
+    ts(span("v16", 0, 512), span("v16", 1024, 1536), T.v16[:, 1024:1536], T.v16[:, 0:512], 1024.0, None, Op.add)
     act(["eye"], ["nd0"], T.nd0[:], T.eye[:], scale=-1 / S0)
-    act(["eye"], ["eyeup"], T.eyeup[:], T.eye[:], scale=UP)
-    act(["eye"], ["ineg"], T.ineg[:], T.eye[:], scale=BIG, bias=-BIG)
     act(["pf", "pm"], ["pg"], col("pg"), col("pm"), scale=-1.0, bias=col("pf"))
     act(["pm"], ["tb"], col("tb"), col("pm"), scale=0.125)
     act(["pg"], ["pg15"], col("pg15"), col("pg"), bias=15.0)
-    act(keys("v16", "uo"), ["sv0"], T.sv0[:], sb("v16", "uo"), scale=S0)
     late = [
-        [lambda: ts(["jj", "pm"], ["rm"], T.rm[:], T.jj[:, 0:16], col("pm"), None, Op.is_equal),
-         lambda: ts(["j16", "pg"], ["grp"], T.grp[:], T.j16[:], col("pg"), None, Op.is_equal)],
-        [lambda: ts(["jj", "pg15"], ["cb0"], T.cb0[:], T.jj[:, 0:144], col("pg15"), BIG, Op.not_equal, Op.mult),
-         lambda: ts(["jj", "pm", "tb"], ["rtb"], T.rtb[:], T.jj[:, 0:16], col("pm"), col("tb"), Op.is_equal, Op.mult)],
-        [lambda: ts(["cb0", "tb"], ["cb"], T.cb[:], T.cb0[:], col("tb"), None, Op.add)],
-        [], [],
+        lambda: ts(["jj", "pg15"], ["cb0"], T.cb0[:], T.jj[:, 0:144], col("pg15"), BIG, Op.not_equal, Op.mult),
+        lambda: ts(["jj", "pm"], ["rm"], T.rm[:], T.jj[:, 0:16], col("pm"), None, Op.is_equal),
+        lambda: ts(["j16", "pg"], ["grp"], T.grp[:], T.j16[:], col("pg"), None, Op.is_equal),
+        lambda: ts(["jj", "pm", "tb"], ["rtb"], T.rtb[:], T.jj[:, 0:16], col("pm"), col("tb"), Op.is_equal, Op.mult),
+        lambda: ts(["cb0", "tb"], ["cb"], T.cb[:], T.cb0[:], col("tb"), None, Op.add),
     ]
 
     def ties():
@@ -229,16 +234,21 @@ def rank_program(g, core, T, topo):
     def side_by_side(n, stop):
         op("t", ["grp", n], ["pe"], PE.matmul, T.pe[:, 0:16], T.grp[:], T[n][:], False, stop)
 
+    def spread(out, key, src, sign):
+        ts(["rm", key], [out], T[out][:], T.rm[:], src, sign, Op.mult, Op.mult)
+
     def least():
         op("v", [], ["pe", "mn"], V.tensor_reduce, col("mn"), T.pe[:, 0:16], X, Op.min)
 
-    def choose(key, own):
-        ts(["cb", "mn", key], ["sel"], T.sel[:], T.cb[:], own, col("mn"), Op.add, Op.is_le)
+    def choose():
+        ts(["cb", "mn", "kk"], ["sel"], T.sel[:], T.cb[:], col("kk"), col("mn"), Op.add, Op.is_le)
 
     def spot(h):
         if h == 0:
             return 0, CS, "pe", T.pe[:, 16:16 + CS // 16]
-        return CS, W, "b0", T.b0[:, 0:(W - CS) // 16]
+        if h == 1:
+            return CS, W, "b0", T.b0[:, 0:(W - CS) // 16]
+        return 0, W, "pe", T.pe[:, 16:16 + K]
 
     def lay(h, sel):
         lo, hi, key, out = spot(h)
@@ -249,47 +259,65 @@ def rank_program(g, core, T, topo):
     def publish(t, h, scale):
         own = T["own%d" % t]
         lo, hi, key, src = spot(h)
-        ts([], [key, "own%d_%d" % (t, h)], own[:, lo // 16:hi // 16], src, scale, -OFF, Op.mult, Op.add)
-        for s in (range(1, F + 1) if h == 1 else []):
+        parts = ["own%d_%d" % (t, j) for j in ((0, 1) if h == 2 else (h,))]
+        ts([], [key] + parts, own[:, lo // 16:hi // 16], src, scale, -OFF, Op.mult, Op.add)
+        for s in (range(1, F + 1) if h else []):
             dst, via = route(T, topo, rank, t, s)
             to, name = (dst, "m%d_%d" % (s, t)) if via is None else (via, "hand%d" % t)
             rid, pid = topo.addr(to, core)
+            mask, n = narrow(T, topo, core, t == 0 and via is not None)
+            sent[0] += n
             op("g", ["own%d_0" % t, "own%d_1" % t], [], g.remote_dma, T[name][:], own[:], T.sem[name], T.sem.sent,
-               pid, rid, emask, dma="sent")
+               pid, rid, mask, dma="sent")
 
-    for c, q in LOADS:
-        mm(c, "eye", "v16", True)
-    for j, (c, q) in enumerate(LOADS):
+    def own_count():
+        op("v", keys("junk", "uo"), ak(UO - 1), V.tensor_tensor_scan, acc(0, UO), sb("junk", "uo"), sb("junk", "uo"),
+           -float(UO), Op.add, Op.add)
+
+    def narrowed(c):
         ts(keys("gi", c), keys("x16", c), sb("x16", c), sb("gi", c), OFF, S0, Op.add, Op.mult)
+
+    act(keys("v16", "uo"), ["sv1"], T.sv1[:], sb("v16", "uo"), bias=-OFF)
+    for c in START:
+        mm(c, "eye", "v16", True)
+    for j, c in enumerate(START):
+        narrowed(c)
         mm(c, "nd0", "x16", False, True)
-        count(c, "c%d" % j, col("c%d" % j))
-        if j < 3:
+        if j < NP - 1:
+            count(c, ak(UO + j)[0], acc(UO + j))
+        else:
+            count(c, "fin", col("fin"))
+        if j < POOLED:
             pool_copy(c, "x32", "x16")
-        for f in late[j]:
+        for f in late[2 * j:2 * j + 2]:
             f()
         if j == 2:
             ties()
-            ahead("a0")
-        if j == 3:
-            ahead("a1")
-    c0 = names.index("c0")
-    op("v", ["c%d" % j for j in range(5)], ak(0), V.tensor_reduce, acc(0), T.col[:, c0:c0 + 5], X, Op.add, negate=True)
-    ts(["rm"] + ak(0), ["rr"], T.rr[:], T.rm[:], acc(0), None, Op.mult)
+    ahead("a1")
+    op("v", keys("gi", "uo") + ["sv1"], keys("junk", "uo"), V.tensor_tensor, sb("junk", "uo"), sb("gi", "uo"), T.sv1[:],
+       Op.is_le)
+    own_count()
+    total("nsb", ak(UO - 1, LIST), acc(UO - 1, LIST), False)
+    spread("rk", "nsb", col("nsb"), 1.0)
+    side_by_side("rk", False)
+    spread("rr", "fin", col("fin"), 1.0)
+    act(["nsb", "fin"], ["kk"], col("kk"), col("fin"), bias=col("nsb"))
     side_by_side("rr", True)
-    for c, q in LOADS[3:]:
+    narrowed("uo")
+    act(["eye"], ["eyeup"], T.eyeup[:], T.eye[:], scale=UP)
+    for c in START[POOLED:] + ("uo",):
         act(keys("x16", c), keys("x32", c), sb("x32", c), sb("x16", c), Act.Copy)
+    act(["eye"], ["ipos"], T.ipos[:], T.eye[:], scale=-BIG, bias=BIG)
+    act(keys("v16", "uo"), ["sv0"], T.sv0[:], sb("v16", "uo"), scale=S0)
+    act(["eye"], ["ineg"], T.ineg[:], T.eye[:], scale=BIG, bias=-BIG)
     least()
-    ahead("u2")
-    choose("acc0", acc(0))
-    for j, x in enumerate((1.0, (UP - 1) / (2 * UP), (UP + 1) / (2 * UP))):
-        op("v", [], ["rsc%d" % j], V.memset, T.rsc[:, j:j + 1], x)
-    lay(0, "sel")
-    lay(1, "sel")
-    publish(0, 0, 1 / S0)
-
-    def gain(k):
-        fin = "fin%d" % (k % 2)
-        ts(["thr", fin], ak(k), acc(k), col("thr"), col(fin), 1.0, Op.subtract, Op.min)
+    ahead("a0")
+    choose()
+    ts(["kk"], ak(LIST), acc(LIST), col("kk"), -1.0, None, Op.mult)
+    lay(2, "sel")
+    publish(0, 2, 1 / S0)
+    for c in ("u2", "u1", "u0a"):
+        ahead(c)
 
     for t in range(RO):
         for s in range(F + 1):
@@ -297,9 +325,10 @@ def rank_program(g, core, T, topo):
             last = t == RO - 1 and s == F
             turn = s == F and not last
             lst = "own%d" % t if s == 0 else "m%d_%d" % (s, t)
-            nd, sv = "nd%d" % s, "sv%d" % s
-            fin, sg = "fin%d" % (k % 2), "sg%d" % s
-            place = [k + 1]
+            nd, sv, psi = "nd%d" % s, "sv%d" % s, "psi%d" % s
+            gain = LIST + k
+            place = [UO]
+            whole = t and not s and "x:a1" not in FIRST
 
             def picked(c):
                 a, b = PIECE[c][0:2]
@@ -308,8 +337,8 @@ def rank_program(g, core, T, topo):
 
             def gather(c):
                 rd, src = picked(c)
-                if c == "u1":
-                    act(rd, keys("dl", c), sb("dl", c), src, Act.Copy, scale=UP)
+                if c in ("u1", "u1a") or (whole and c == "a1"):
+                    act(rd, keys("dl", c), sb("dl", c), src, Act.Copy, scale=UP if c[0] == "u" else 1.0)
                 elif c[0] == "u":
                     ts(rd, keys("dl", c), sb("dl", c), src, UP, None, Op.mult)
                 else:
@@ -318,19 +347,23 @@ def rank_program(g, core, T, topo):
 
             def tally(c):
                 mm(c, nd, "dl", False, True)
-                if place[0] < k + NP:
+                if place[0] < LIST:
                     count(c, ak(place[0])[0], acc(place[0]))
                 else:
-                    count(c, fin, col(fin))
+                    count(c, "fin", col("fin"))
                 place[0] += 1
 
-            for what, c in (x.split(":") for x in (PHASE if s else FIRST)):
+            for what, c in (x.split(":") for x in (FIRST if t and not s else PHASE)):
                 if what == "g":
                     gather(c)
                 elif what == "c":
                     tally(c)
                 elif what == "p":
-                    publish(t, 1, 1.0 if t else 1 / S0)
+                    publish(t, 1, 1.0)
+                elif what == "n":
+                    if s:
+                        was = ("nd%d" % (s - 1), "psi%d" % (s - 1))
+                        ts(was, [nd], T[nd][:], T[was[0]][:], col(was[1]), None, Op.mult)
                 elif what == "x" and c[0] == "a":
                     mm(c, nd, "x16")
                 elif what == "x":
@@ -338,58 +371,72 @@ def rank_program(g, core, T, topo):
                 elif not (last and c[0] == "a"):
                     ahead(c)
             rd, src = picked("uo")
-            op("v", rd + [sv], keys("junk", "uo"), V.tensor_tensor, sb("junk", "uo"), src, T[sv][:], Op.is_gt)
-            if s:
-                gain(k - 1)
-            op("v", keys("junk", "uo"), ["n1"], V.tensor_reduce, col("n1"), sb("junk", "uo"), X, Op.add)
-            if last:
-                ts(["psi0"], ["psi0"], col("psi0"), col("psi0"), 1 / S0, None, Op.mult)
-            if s == F:
-                op("v", ak(0, k), ["nsb"], V.tensor_reduce, col("nsb"), acc(0, k), X, Op.add)
-            ts(["n1"], ak(k), acc(k), col("n1"), 2.0, -float(UO), Op.mult, Op.add)
-            if s == F:
-                ts(["rsc0", "rsc1", "rsc2", "psi0", "psi1"], ["rs"], T.rs[:, 0:3], T.rsc[:, 0:3], col("psi0"),
-                   col("psi1"), Op.mult, Op.mult)
+            op("v", rd + [sv], keys("junk", "uo"), V.tensor_tensor, sb("junk", "uo"), src, T[sv][:], Op.is_le)
+            if last or (s == F and "n:rho" not in POST):
+                ts(["psi0", "psi1"], ["rho"], col("rho"), col("psi0"), col("psi1"), 1 / S0 if last else 1.0,
+                   Op.mult, Op.mult)
+            own_count()
             if turn:
-                ts(["rm", "nsb"], ["rk"], T.rk[:], T.rm[:], col("nsb"), None, Op.mult)
-                ts(["nsb"], ["nsk"], col("nsk"), col("nsb"), -16.0, None, Op.add)
+                if "n:rk" not in POST:
+                    spread("rk", "nsb", col("nsb"), 1.0)
                 ties()
                 side_by_side("rk", False)
-            op("v", ak(0, k + NP + 1), ["thr"], V.tensor_reduce, col("thr"), acc(0, k + NP + 1), X, Op.add, negate=True)
-
-            def take():
-                ts(["ineg", fin, "thr"], ["take"], T.take[:], T.ineg[:], col(fin), col("thr"), Op.add, Op.is_gt)
+            total("thr", ak(UO - 1, gain), acc(UO - 1, gain), True)
 
             def larger(c, out):
                 op("v", keys("x32", c), [bk(c)] + keys(out, c), V.tensor_tensor, sb(out, c), sb("x32", c), ps(c), Op.max)
 
             def after(c):
+                if whole and c == "b1":
+                    mm(c, "keep", "x16", True)
                 mm(c, "take", "dl", c[0] == "u", True)
 
-            act([fin, "thr"], [sg], col(sg), col(fin), Act.Sign, bias=col("thr"), scale=-1.0)
+            def shrink():
+                act(["tk"], [psi], col(psi), col("tk"), bias=1.0, scale=-(UP - 1) / UP)
+
+            act(["fin", "thr"], ak(gain), acc(gain), col("fin"), Act.Relu, bias=col("thr"), scale=-1.0)
+            act(ak(gain), ["tk"], col("tk"), acc(gain), Act.Sign)
+            ts(["ipos", "fin", "thr"], ["take"], T.take[:], T.ipos[:], col("fin"), col("thr"), Op.add, Op.is_lt)
             if s < F:
-                psi = "psi%d" % s
-                act([sg], ["phi"], col("phi"), col(sg), bias=(UP + 1) / 2, scale=-(UP - 1) / 2)
-                act([sg], [psi], col(psi), col(sg), bias=(UP + 1) / (2 * UP), scale=(UP - 1) / (2 * UP))
-                take()
+                act(["tk"], ["phi"], col("phi"), col("tk"), bias=1.0, scale=UP - 1)
                 gather("uo")
-                for c in POST:
-                    after(c)
-                    if c[0] == "u":
+                if whole:
+                    ts(["ineg", "fin", "thr"], ["keep"], T.keep[:], T.ineg[:], col("fin"), col("thr"), Op.add, Op.is_ge)
+                if s == F - 1:
+                    total("nsb", ak(LIST, gain + 1), acc(LIST, gain + 1), True)
+                for what, c in (x.split(":") for x in POST):
+                    if what == "t":
+                        after(c)
+                    elif what == "v":
+                        ahead(c)
+                    elif c == "psi":
+                        shrink()
+                    elif c == "nd":
+                        ts([nd, psi], ["nd%d" % (s + 1)], T["nd%d" % (s + 1)][:], T[nd][:], col(psi), None, Op.mult)
+                    elif c == "rho":
+                        if s == F - 1 and t < RO - 1:
+                            act(["psi0", psi], ["rho"], col("rho"), col(psi), Act.Copy, scale=col("psi0"))
+                    elif c == "rk":
+                        if s == F - 1 and t < RO - 1:
+                            act(["rm", "nsb"], ["rk"], T.rk[:], T.rm[:], Act.Copy, scale=col("nsb"))
+                    elif c == "sv":
+                        act([sv, "phi"], ["sv%d" % (s + 1)], T["sv%d" % (s + 1)][:], T[sv][:], Act.Copy,
+                            scale=col("phi"))
+                    elif c[0] == "u":
                         larger(c, "x32")
                     else:
                         act(["phi"], [c] + keys("x32", c), sb("x32", c), ps(c), Act.Copy, scale=col("phi"))
                         pool_copy(c, "x16", "x32")
-                    if c == POST[0]:
-                        ts([nd, psi], ["nd%d" % (s + 1)], T["nd%d" % (s + 1)][:], T[nd][:], col(psi), None, Op.mult)
-                act([sv, "phi"], ["sv%d" % (s + 1)], T["sv%d" % (s + 1)][:], T[sv][:], Act.Copy, scale=col("phi"))
-                for c in AHEAD:
-                    ahead(c)
                 continue
 
-            act([sg, "rs"], ["w"], col("w"), col(sg), bias=T.rs[:, 2:3], scale=T.rs[:, 1:2])
+            def own_key():
+                act(ak(gain) + ["nsb"], ["kk"], col("kk"), acc(gain), scale=-1.0, bias=col("nsb"))
+
+            def scale_after():
+                shrink()
+                act([psi, "rho"], ["w"], col("w"), col(psi), Act.Copy, scale=col("rho"))
+
             if last:
-                take()
                 gather("uo")
 
                 def store(c):
@@ -397,24 +444,30 @@ def rank_program(g, core, T, topo):
 
                 for c in ("b1", "b0", "u2", "u1", "u0"):
                     after(c)
-                ts(["rs"], ["b1"] + keys("x32", "b1"), sb("x32", "b1"), ps("b1"), T.rs[:, 0:1], -OFF, Op.mult, Op.add)
+                own_key()
+                shrink()
+                act(["kk"], ["ecol"], T.ecol[:], col("kk"), scale=-0.5, bias=W / 2)
+                ts(["rho"], ["b1"] + keys("x32", "b1"), sb("x32", "b1"), ps("b1"), col("rho"), -OFF, Op.mult, Op.add)
                 store("b1")
-                act(["rs"], ["b0"] + keys("x32", "b0"), sb("x32", "b0"), ps("b0"), bias=-OFF, scale=T.rs[:, 0:1])
+                act(["rho"], ["b0"] + keys("x32", "b0"), sb("x32", "b0"), ps("b0"), bias=-OFF, scale=col("rho"))
                 store("b0")
-                gain(k)
+                act([psi, "rho"], ["w"], col("w"), col(psi), Act.Copy, scale=col("rho"))
+                op("t", ["ecol", "eye"], ["pe"], PE.matmul, T.pe[0:1, 0:128], T.ecol[:], T.eye[:], True, True)
                 for c in ("u2", "u1", "u0"):
                     larger(c, "x16")
+                for c in ("u2", "u1", "uo"):
                     act(["w"] + keys("x16", c), keys("x32", c), sb("x32", c), sb("x16", c), bias=-OFF, scale=col("w"))
-                    store(c)
-                    if c == "u2":
-                        ts(ak(k) + ["nsb"], ["kk"], col("kk"), acc(k), col("nsb"), -float(W + k), Op.add, Op.add)
-                    if c == "u1":
-                        ts(["kk"], ["ecol"], T.ecol[:], col("kk"), -0.5, None, Op.mult)
-                        op("g", ["ecol"], [], g.dma_start, T.ye[:], T.ecol[:], dma="ste", allow_slow_non_contiguous=True)
+                    if c != "uo":
+                        store(c)
+                ts(["w"] + keys("x16", "u0a"), keys("x32", "u0a"), sb("x32", "u0a"), sb("x16", "u0a"), col("w"), -OFF,
+                   Op.mult, Op.add)
+                store("u0")
+                act([], ["pe", "erow"], T.erow[0:1, :], T.pe[0:1, 0:128], Act.Copy)
+                op("s", ["erow"], [], S.dma_start, T.ye[:, 0], T.erow[0:1, :], dma="st")
                 continue
 
             def plain(c, out):
-                act(["rs"], [c] + keys(out, c), sb(out, c), ps(c), Act.Copy, scale=T.rs[:, 0:1])
+                act(["rho"], [c] + keys(out, c), sb(out, c), ps(c), Act.Copy, scale=col("rho"))
 
             def level(q, c):
                 if q == "s":
@@ -422,36 +475,29 @@ def rank_program(g, core, T, topo):
                 else:
                     ts(["w"] + keys("x16", c), keys("x32", c), sb("x32", c), sb("x16", c), col("w"), None, Op.mult)
 
-            take()
-            gain(k)
-            gather("uo")
-            ts(["rm"] + ak(k), ["rr"], T.rr[:], T.rm[:], acc(k), -1.0, Op.mult, Op.add)
-            act(ak(k) + ["nsk"], ["kk"], col("kk"), acc(k), bias=col("nsk"))
-            after("b0")
-            after("u2")
-            side_by_side("rr", True)
-            after("b1")
-            after("u1")
-            after("u0")
-            plain("b0", "x16")
-            pool_copy("b0", "x32", "x16")
-            least()
-            larger("u2", "x16")
-            plain("b1", "x16")
-            choose("kk", col("kk"))
-            larger("u1", "x16")
-            larger("u0", "x16")
-            ts(["sel", "w"], ["selu"], T.selu[:], T.sel[:], col("w"), 1 / S0, Op.mult, Op.mult)
-            ahead("u2")
-            lay(0, "sel")
-            plain("b1", "x32")
-            level("s", "u2")
-            level("s", "u1")
-            lay(1, "selu")
-            level("v", "u0")
-            publish(t + 1, 0, 1 / S0)
+            once = {"rr": lambda: spread("rr", ak(gain)[0], acc(gain), -1.0), "kk": own_key, "w": scale_after,
+                    "side": lambda: side_by_side("rr", True), "min": least, "sel": choose,
+                    "selu": lambda: ts(["sel", "w"], ["selu"], T.selu[:], T.sel[:], col("w"), 1 / S0, Op.mult, Op.mult),
+                    "lay0": lambda: lay(0, "sel"), "lay1": lambda: lay(1, "selu"),
+                    "own0": lambda: publish(t + 1, 0, 1 / S0)}
+            for what, c in (x.split(":") for x in TURN):
+                if what == "e":
+                    once[c]()
+                elif what == "g":
+                    gather(c)
+                elif what == "t":
+                    after(c)
+                elif what == "v":
+                    ahead(c)
+                elif what == "h":
+                    larger(c, "x16") if c[0] == "u" else plain(c, "x16")
+                elif what == "G":
+                    pool_copy(c, "x32", "x16")
+                elif c[0] == "b":
+                    plain(c, "x32")
+                else:
+                    level(what.lower(), c)
 
     done = emit(g, T, ops, ext)
     g.sync.wait_ge(T.sem.st, done["st"])
-    g.wait_ge(T.sem.ste, done["ste"])
-    g.wait_ge(T.sem.sent, RO * F * en)
+    g.wait_ge(T.sem.sent, sent[0])

from concourse.mybir import AluOpType as Op, AxisListType, ActivationFunctionType as Act

W, RO, F, N = 2016, 3, 2, 8
K = W // 16
OFF, UP = 32.0, 64.0
S0 = 2.0 ** -14
BIG = 30000.0
A0, A1, B0 = 448, 352, 448
U2, U1, U0A, U0B = 256, 480, 288, 0
U1A = 160
CS = A0 + A1
C2, C1 = CS + U2, CS + U2 + U1
PIECE = {"a0": (0, A0, "a0"), "a1": (A0, CS, "a1"), "b0": (0, B0, "b0"), "b1": (B0, CS, "b1"),
         "u2": (CS, C2, "u2"), "u1": (C2, C1, "u1"), "u0": (C1, W, "u0"),
         "u0a": (C1, C1 + U0A, "u0"), "u0b": (C1 + U0A, C1 + U0A + U0B, "u0"), "uo": (C1 + U0A + U0B, W, "u0"),
         "u1a": (C2, C2 + U1A, "u1"), "u1b": (C2 + U1A, C1, "u1")}
BASE = {n: PIECE[n][0] for n in ("a0", "a1", "b0", "b1", "u2", "u1", "u0")}
UO = W - PIECE["uo"][0]
PHASE = ("g:u1 g:u2 g:u0a g:a0 g:a1 c:u2 c:u1 c:u0a x:b0 x:a0 c:a0 x:a1 c:a1 x:b1 v:a0").split()
FIRST = ("g:a0 g:a1 p:1 g:u1a g:u1b g:u0a g:u2 x:a0 c:a1 c:a0 v:u1 c:u1 v:u0a c:u0a x:b0 c:u2 v:a0").split()
POST = ("t:u1 t:b0 t:u0 t:u2 t:b1 n:psi n:sv w:u1 w:b0 w:u0 w:u2 w:b1 n:nd v:u1 v:a1 v:u0a v:u2").split()
TURN = ("e:rr g:uo e:kk v:a1 t:b0 e:side t:u2 t:b1 t:u1 t:u0 e:min h:u2 h:b0 h:b1 e:w G:b0 e:sel h:u1 S:b1 S:u1 S:u2 h:u0 v:u2 e:lay0 e:selu e:lay1 V:u0 e:own0").split()
NP = sum(x[0] == "c" for x in PHASE)
LOADS = [("a1", "y"), ("u1", "s"), ("a0", "y"), ("u0a", "s"), ("u2", "y"), ("uo", "s")]
START = ("a1", "u1", "a0", "u0a", "u2")
POOLED = 3
LIST = UO + NP - 1

SCRATCH = {
    "gi": ("sbuf", [128, W], "int32"),
    "x32": ("sbuf", [128, W], "float32"),
    "x16": ("sbuf", [128, W], "float16"),
    "dl": ("sbuf", [128, W], "float16"),
    "v16": ("sbuf", [128, W], "float16"),
    "junk": ("sbuf", [128, W], "bfloat16"),
    "jj": ("sbuf", [128, 256], "float32"),
    "j16": ("sbuf", [128, 128], "float32"),
    "pint": ("sbuf", [128, 2], "int32"),
    "col": ("sbuf", [128, 32], "float32"),
    "acc": ("sbuf", [128, LIST + 16], "float32"),
    "ecol": ("sbuf", [128, 1], "float16"),
    "erow": ("sbuf", [128, 128], "float32"),
    "rm": ("sbuf", [128, 16], "float16"),
    "rtb": ("sbuf", [128, 16], "float16"),
    "rk": ("sbuf", [128, 16], "float16"),
    "rr": ("sbuf", [128, 16], "float16"),
    "pe": ("psum", [128, 512], "float32"),
}
for _n in ("eye", "eyeup", "ipos", "ineg", "take", "keep", "grp", "nd0", "nd1", "nd2"):
    SCRATCH[_n] = ("sbuf", [128, 128], "float16")
for _n in ("cb0", "cb", "sel", "selu"):
    SCRATCH[_n] = ("sbuf", [128, 144], "float16")
for _n in ("sv0", "sv1", "sv2"):
    SCRATCH[_n] = ("sbuf", [128, UO], "float16")
for _n in BASE:
    SCRATCH[_n] = ("psum", [128, 512], "float32")
for _t in range(RO):
    for _n in ("own", "hand", "m1_", "m2_"):
        SCRATCH["%s%d" % (_n, _t)] = ("sbuf", [128, K], "uint16")

SEMAPHORES = (["cv", "cs", "ct", "cg", "st", "sent"] + ["ld%d" % k for k in range(len(LOADS))]
              + ["%s%d" % (n, t) for t in range(RO) for n in ("hand", "m1_", "m2_")])


def route(T, topo, r, t, s):
    src = T.cores[r]
    dst = T.cores[(r - 1 - (F * t + s - 1) % (N - 1)) % N]
    if topo.may_write(src, dst):
        return dst, None
    able = [c for c in topo.cores_of(src) if T.rank_of(c) is None and topo.may_write(c, dst)]
    near = [c for c in able if topo.die(c) == topo.die(src)]
    return dst, (near or able)[0]


def narrow(T, topo, core, half=False):
    far = [c for c in T.cores if c not in topo.cores_of(core) and topo.may_write(core, c)]
    eng = topo.engines(core, far[0])
    return sum(1 << e for e in eng), len(eng)


def arrivals(T, topo, r, t, s):
    q = (r + 1 + (F * t + s - 1) % (N - 1)) % N
    dst, via = route(T, topo, q, t, s)
    return narrow(T, topo, T.cores[q])[1] if via is None else narrow(T, topo, via, t == 0)[1]


def relay_program(g, core, T, topo):
    sent = 0
    for t in range(RO):
        for s in range(1, F + 1):
            for r in range(N):
                dst, via = route(T, topo, r, t, s)
                if via != core:
                    continue
                mask, n = narrow(T, topo, core, t == 0)
                g.wait_ge(T.sem["hand%d" % t], narrow(T, topo, T.cores[r], t == 0)[1])
                rid, pid = topo.addr(dst, core)
                g.remote_dma(T["m%d_%d" % (s, t)][:], T["hand%d" % t][:], T.sem["m%d_%d" % (s, t)], T.sem.sent,
                             pid, rid, mask)
                sent += n
    if sent:
        g.wait_ge(T.sem.sent, sent)


def emit(g, T, ops, ext):
    queues = {"v": g.vector, "s": g.scalar, "t": g.tensor, "g": g, "y": g.sync}
    writer, readers, known, clock, waits, needed = {}, {}, {q: {} for q in queues}, [], [], set()
    chain = lambda i: ops[i][4] or "c" + ops[i][0]
    for i, (q, call, rd, wr, dma) in enumerate(ops):
        deps = set(writer[k] for k in rd + wr if k in writer)
        for k in wr:
            deps.update(readers.get(k, []))
        mine = []
        for k in rd:
            if k in ext and ext[k][0] not in known[q]:
                known[q][ext[k][0]] = 0
                mine.append(ext[k])
        for d in sorted(deps, reverse=True):
            if q == "t" and ops[d][0] == "t":
                continue
            if known[q].get(chain(d), -1) >= d:
                continue
            needed.add(d)
            mine.append(d)
            for c, x in clock[d].items():
                known[q][c] = max(known[q].get(c, -1), x)
        waits.append(mine)
        mark = dict(known[q])
        mark[chain(i)] = i
        clock.append(mark)
        for k in wr:
            writer[k] = i
            readers[k] = []
        for k in rd:
            readers.setdefault(k, []).append(i)
    count, value = {}, {}
    for i, (q, call, rd, wr, dma) in enumerate(ops):
        for d in waits[i]:
            if isinstance(d, tuple):
                queues[q].wait_ge(T.sem[d[0]], d[1])
            else:
                queues[q].wait_ge(T.sem[chain(d)], value[d])
        ins = call()
        if dma == "sent":
            continue
        if dma or i in needed:
            n = 16 if dma else 1
            count[chain(i)] = value[i] = count.get(chain(i), 0) + n
            ins.then_inc(T.sem[chain(i)], n)
    return count


def rank_program(g, core, T, topo):
    rank = T.rank_of(core)
    if rank is None:
        relay_program(g, core, T, topo)
        return
    V, S, PE = g.vector, g.scalar, g.tensor
    X = AxisListType.X
    ops = []
    ext = {"m%d_%d" % (s, t): ("m%d_%d" % (s, t), arrivals(T, topo, rank, t, s))
           for t in range(RO) for s in range(1, F + 1)}
    sent = [0]
    span = lambda n, a, b: ["%s:%d" % (n, j) for j in range(a // 32, (b + 31) // 32)]
    keys = lambda n, c: span(n, PIECE[c][0], PIECE[c][1])
    sb = lambda n, c: T[n][:, PIECE[c][0]:PIECE[c][1]]
    bk = lambda c: PIECE[c][2]
    ps = lambda c: T[bk(c)][:, PIECE[c][0] - BASE[bk(c)]:PIECE[c][1] - BASE[bk(c)]]
    names = ["pf", "pm", "pg", "pg15", "tb", "thr", "mn", "kk", "nsb", "phi", "w", "wu", "rho", "fin", "tk",
             "psi0", "psi1", "psi2", "c0", "c1", "c2", "c3", "c4", "c5"]
    col = lambda n: T.col[:, names.index(n):names.index(n) + 1]
    acc = lambda a, b=None: T.acc[:, a:(a + 1 if b is None else b)]
    ak = lambda a, b=None: ["acc%d" % j for j in range(a, a + 1 if b is None else b)]

    def op(q, rd, wr, fn, *args, dma=None, **kw):
        ops.append((q, lambda: fn(*args, **kw), list(rd), list(wr), dma))

    def ts(rd, wr, out, in0, s1, s2, o0, o1=None):
        if o1 is None:
            op("v", rd, wr, V.tensor_scalar, out, in0, s1, None, o0)
        else:
            op("v", rd, wr, V.tensor_scalar, out, in0, s1, s2, o0, o1)

    def act(rd, wr, out, in_, fn=Act.Identity, **kw):
        op("s", rd, wr, S.activation, out, in_, fn, **kw)

    def mm(c, lhs, rhs, start=False, stop=False):
        op("t", [lhs] + keys(rhs, c), [bk(c)], PE.matmul, ps(c), T[lhs][:], sb(rhs, c), start, stop)

    def ahead(c):
        mm(c, "eyeup" if c[0] == "u" else "eye", "v16", True)

    def count(c, key, out):
        act([], [bk(c), key] + keys("junk", c), sb("junk", c), ps(c), Act.Sign, bias=0.5, accum_out=out)

    def pool_copy(c, out, in_):
        op("g", keys(in_, c), keys(out, c), g.affine_select, sb(out, c), sb(in_, c),
           [[0, PIECE[c][1] - PIECE[c][0]]], Op.is_ge, 0.0, 0, 0)

    def total(out, rd, src, negate):
        op("v", rd, [out], V.tensor_reduce, col(out), src, X, Op.add, negate=negate)

    for k, (c, q) in enumerate(LOADS):
        op(q, [], keys("gi", c), (S if q == "s" else g.sync).dma_start, sb("gi", c), sb("g0", c), dma="ld%d" % k)
    loose = dict(allow_small_or_imprecise_dtypes=True)
    op("g", [], ["jj"], g.iota, T.jj[:], [[1, 256]], 0, 0, **loose)
    op("g", [], ["pint0"], g.iota, T.pint[:, 0:1], [[0, 1]], 0, 1)
    op("g", [], ["j16"], g.iota, T.j16[:], [[16, 8], [0, 16]], 0, 0, **loose)
    J = T.jj[:, 0:128]
    ts(["jj"], span("v16", 0, 256), T.v16[:, 0:256], T.jj[:], OFF, None, Op.add)
    act(["jj"], span("v16", 256, 512), T.v16[:, 256:512], T.jj[:], bias=256.0 + OFF)
    op("v", ["pint0"], ["pf"], V.tensor_copy, col("pf"), T.pint[:, 0:1])
    ts(["pint0"], ["pint1"], T.pint[:, 1:2], T.pint[:, 0:1], 15, None, Op.bitwise_and)
    ts(span("v16", 0, 512), span("v16", 512, 1024), T.v16[:, 512:1024], T.v16[:, 0:512], 512.0, None, Op.add)
    act(span("v16", 0, 480), span("v16", 1536, W), T.v16[:, 1536:W], T.v16[:, 0:W - 1536], bias=1536.0)
    ts(["jj", "pf"], ["eye"], T.eye[:], J, col("pf"), None, Op.is_equal)
    op("v", ["pint1"], ["pm"], V.tensor_copy, col("pm"), T.pint[:, 1:2])
    ts(span("v16", 0, 512), span("v16", 1024, 1536), T.v16[:, 1024:1536], T.v16[:, 0:512], 1024.0, None, Op.add)
    act(["eye"], ["nd0"], T.nd0[:], T.eye[:], scale=-1 / S0)
    act(["pf", "pm"], ["pg"], col("pg"), col("pm"), scale=-1.0, bias=col("pf"))
    act(["pm"], ["tb"], col("tb"), col("pm"), scale=0.125)
    act(["pg"], ["pg15"], col("pg15"), col("pg"), bias=15.0)
    late = [
        lambda: ts(["jj", "pg15"], ["cb0"], T.cb0[:], T.jj[:, 0:144], col("pg15"), BIG, Op.not_equal, Op.mult),
        lambda: ts(["jj", "pm"], ["rm"], T.rm[:], T.jj[:, 0:16], col("pm"), None, Op.is_equal),
        lambda: ts(["j16", "pg"], ["grp"], T.grp[:], T.j16[:], col("pg"), None, Op.is_equal),
        lambda: ts(["jj", "pm", "tb"], ["rtb"], T.rtb[:], T.jj[:, 0:16], col("pm"), col("tb"), Op.is_equal, Op.mult),
        lambda: ts(["cb0", "tb"], ["cb"], T.cb[:], T.cb0[:], col("tb"), None, Op.add),
    ]

    def ties():
        op("t", ["grp", "rtb"], ["pe"], PE.matmul, T.pe[:, 0:16], T.grp[:], T.rtb[:], True, False)

    def side_by_side(n, stop):
        op("t", ["grp", n], ["pe"], PE.matmul, T.pe[:, 0:16], T.grp[:], T[n][:], False, stop)

    def spread(out, key, src, sign):
        ts(["rm", key], [out], T[out][:], T.rm[:], src, sign, Op.mult, Op.mult)

    def least():
        op("v", [], ["pe", "mn"], V.tensor_reduce, col("mn"), T.pe[:, 0:16], X, Op.min)

    def choose():
        ts(["cb", "mn", "kk"], ["sel"], T.sel[:], T.cb[:], col("kk"), col("mn"), Op.add, Op.is_le)

    def spot(h):
        if h == 0:
            return 0, CS, "pe", T.pe[:, 16:16 + CS // 16]
        if h == 1:
            return CS, W, "b0", T.b0[:, 0:(W - CS) // 16]
        return 0, W, "pe", T.pe[:, 16:16 + K]

    def lay(h, sel):
        lo, hi, key, out = spot(h)
        for a in range(16):
            op("t", [sel] + span("x16", lo, hi), [key], PE.matmul, out, T[sel][:, 15 - a:143 - a],
               T.x16[:, lo + a:hi:16], a == 0, a == 15)

    def publish(t, h, scale):
        own = T["own%d" % t]
        lo, hi, key, src = spot(h)
        parts = ["own%d_%d" % (t, j) for j in ((0, 1) if h == 2 else (h,))]
        ts([], [key] + parts, own[:, lo // 16:hi // 16], src, scale, -OFF, Op.mult, Op.add)
        for s in (range(1, F + 1) if h else []):
            dst, via = route(T, topo, rank, t, s)
            to, name = (dst, "m%d_%d" % (s, t)) if via is None else (via, "hand%d" % t)
            rid, pid = topo.addr(to, core)
            mask, n = narrow(T, topo, core, t == 0 and via is not None)
            sent[0] += n
            op("g", ["own%d_0" % t, "own%d_1" % t], [], g.remote_dma, T[name][:], own[:], T.sem[name], T.sem.sent,
               pid, rid, mask, dma="sent")

    def own_count():
        op("v", keys("junk", "uo"), ak(UO - 1), V.tensor_tensor_scan, acc(0, UO), sb("junk", "uo"), sb("junk", "uo"),
           -float(UO), Op.add, Op.add)

    def narrowed(c):
        ts(keys("gi", c), keys("x16", c), sb("x16", c), sb("gi", c), OFF, S0, Op.add, Op.mult)

    act(keys("v16", "uo"), ["sv1"], T.sv1[:], sb("v16", "uo"), bias=-OFF)
    for c in START:
        mm(c, "eye", "v16", True)
    for j, c in enumerate(START):
        narrowed(c)
        mm(c, "nd0", "x16", False, True)
        if j < NP - 1:
            count(c, ak(UO + j)[0], acc(UO + j))
        else:
            count(c, "fin", col("fin"))
        if j < POOLED:
            pool_copy(c, "x32", "x16")
        for f in late[2 * j:2 * j + 2]:
            f()
        if j == 2:
            ties()
    ahead("a1")
    op("v", keys("gi", "uo") + ["sv1"], keys("junk", "uo"), V.tensor_tensor, sb("junk", "uo"), sb("gi", "uo"), T.sv1[:],
       Op.is_le)
    own_count()
    total("nsb", ak(UO - 1, LIST), acc(UO - 1, LIST), False)
    spread("rk", "nsb", col("nsb"), 1.0)
    side_by_side("rk", False)
    spread("rr", "fin", col("fin"), 1.0)
    act(["nsb", "fin"], ["kk"], col("kk"), col("fin"), bias=col("nsb"))
    side_by_side("rr", True)
    narrowed("uo")
    act(["eye"], ["eyeup"], T.eyeup[:], T.eye[:], scale=UP)
    for c in START[POOLED:] + ("uo",):
        act(keys("x16", c), keys("x32", c), sb("x32", c), sb("x16", c), Act.Copy)
    act(["eye"], ["ipos"], T.ipos[:], T.eye[:], scale=-BIG, bias=BIG)
    act(keys("v16", "uo"), ["sv0"], T.sv0[:], sb("v16", "uo"), scale=S0)
    act(["eye"], ["ineg"], T.ineg[:], T.eye[:], scale=BIG, bias=-BIG)
    least()
    ahead("a0")
    choose()
    ts(["kk"], ak(LIST), acc(LIST), col("kk"), -1.0, None, Op.mult)
    lay(2, "sel")
    publish(0, 2, 1 / S0)
    for c in ("u2", "u1", "u0a"):
        ahead(c)

    for t in range(RO):
        for s in range(F + 1):
            k = 3 * t + s + 1
            last = t == RO - 1 and s == F
            turn = s == F and not last
            lst = "own%d" % t if s == 0 else "m%d_%d" % (s, t)
            nd, sv, psi = "nd%d" % s, "sv%d" % s, "psi%d" % s
            gain = LIST + k
            place = [UO]
            whole = t and not s and "x:a1" not in FIRST

            def picked(c):
                a, b = PIECE[c][0:2]
                rd = span("x32", 0, W) + [lst if s else "%s_%d" % (lst, int(a >= CS))]
                return rd, T.x32[:, 0:W].indirect(T[lst][:, a // 16:b // 16])

            def gather(c):
                rd, src = picked(c)
                if c in ("u1", "u1a") or (whole and c == "a1"):
                    act(rd, keys("dl", c), sb("dl", c), src, Act.Copy, scale=UP if c[0] == "u" else 1.0)
                elif c[0] == "u":
                    ts(rd, keys("dl", c), sb("dl", c), src, UP, None, Op.mult)
                else:
                    op("v", rd + keys("x16", c), keys("dl", c), V.tensor_tensor, sb("dl", c), src, sb("x16", c),
                       Op.subtract)

            def tally(c):
                mm(c, nd, "dl", False, True)
                if place[0] < LIST:
                    count(c, ak(place[0])[0], acc(place[0]))
                else:
                    count(c, "fin", col("fin"))
                place[0] += 1

            for what, c in (x.split(":") for x in (FIRST if t and not s else PHASE)):
                if what == "g":
                    gather(c)
                elif what == "c":
                    tally(c)
                elif what == "p":
                    publish(t, 1, 1.0)
                elif what == "n":
                    if s:
                        was = ("nd%d" % (s - 1), "psi%d" % (s - 1))
                        ts(was, [nd], T[nd][:], T[was[0]][:], col(was[1]), None, Op.mult)
                elif what == "x" and c[0] == "a":
                    mm(c, nd, "x16")
                elif what == "x":
                    mm(c, "eye", "x16", True)
                elif not (last and c[0] == "a"):
                    ahead(c)
            rd, src = picked("uo")
            op("v", rd + [sv], keys("junk", "uo"), V.tensor_tensor, sb("junk", "uo"), src, T[sv][:], Op.is_le)
            if last or (s == F and "n:rho" not in POST):
                ts(["psi0", "psi1"], ["rho"], col("rho"), col("psi0"), col("psi1"), 1 / S0 if last else 1.0,
                   Op.mult, Op.mult)
            own_count()
            if turn:
                if "n:rk" not in POST:
                    spread("rk", "nsb", col("nsb"), 1.0)
                ties()
                side_by_side("rk", False)
            total("thr", ak(UO - 1, gain), acc(UO - 1, gain), True)

            def larger(c, out):
                op("v", keys("x32", c), [bk(c)] + keys(out, c), V.tensor_tensor, sb(out, c), sb("x32", c), ps(c), Op.max)

            def after(c):
                if whole and c == "b1":
                    mm(c, "keep", "x16", True)
                mm(c, "take", "dl", c[0] == "u", True)

            def shrink():
                act(["tk"], [psi], col(psi), col("tk"), bias=1.0, scale=-(UP - 1) / UP)

            act(["fin", "thr"], ak(gain), acc(gain), col("fin"), Act.Relu, bias=col("thr"), scale=-1.0)
            act(ak(gain), ["tk"], col("tk"), acc(gain), Act.Sign)
            ts(["ipos", "fin", "thr"], ["take"], T.take[:], T.ipos[:], col("fin"), col("thr"), Op.add, Op.is_lt)
            if s < F:
                act(["tk"], ["phi"], col("phi"), col("tk"), bias=1.0, scale=UP - 1)
                gather("uo")
                if whole:
                    ts(["ineg", "fin", "thr"], ["keep"], T.keep[:], T.ineg[:], col("fin"), col("thr"), Op.add, Op.is_ge)
                if s == F - 1:
                    total("nsb", ak(LIST, gain + 1), acc(LIST, gain + 1), True)
                for what, c in (x.split(":") for x in POST):
                    if what == "t":
                        after(c)
                    elif what == "v":
                        ahead(c)
                    elif c == "psi":
                        shrink()
                    elif c == "nd":
                        ts([nd, psi], ["nd%d" % (s + 1)], T["nd%d" % (s + 1)][:], T[nd][:], col(psi), None, Op.mult)
                    elif c == "rho":
                        if s == F - 1 and t < RO - 1:
                            act(["psi0", psi], ["rho"], col("rho"), col(psi), Act.Copy, scale=col("psi0"))
                    elif c == "rk":
                        if s == F - 1 and t < RO - 1:
                            act(["rm", "nsb"], ["rk"], T.rk[:], T.rm[:], Act.Copy, scale=col("nsb"))
                    elif c == "sv":
                        act([sv, "phi"], ["sv%d" % (s + 1)], T["sv%d" % (s + 1)][:], T[sv][:], Act.Copy,
                            scale=col("phi"))
                    elif c[0] == "u":
                        larger(c, "x32")
                    else:
                        act(["phi"], [c] + keys("x32", c), sb("x32", c), ps(c), Act.Copy, scale=col("phi"))
                        pool_copy(c, "x16", "x32")
                continue

            def own_key():
                act(ak(gain) + ["nsb"], ["kk"], col("kk"), acc(gain), scale=-1.0, bias=col("nsb"))

            def scale_after():
                shrink()
                act([psi, "rho"], ["w"], col("w"), col(psi), Act.Copy, scale=col("rho"))

            if last:
                gather("uo")

                def store(c):
                    op("y", keys("x32", c), [], g.sync.dma_start, sb("yg", c), sb("x32", c), dma="st")

                for c in ("b1", "b0", "u2", "u1", "u0"):
                    after(c)
                own_key()
                shrink()
                act(["kk"], ["ecol"], T.ecol[:], col("kk"), scale=-0.5, bias=W / 2)
                ts(["rho"], ["b1"] + keys("x32", "b1"), sb("x32", "b1"), ps("b1"), col("rho"), -OFF, Op.mult, Op.add)
                store("b1")
                act(["rho"], ["b0"] + keys("x32", "b0"), sb("x32", "b0"), ps("b0"), bias=-OFF, scale=col("rho"))
                store("b0")
                act([psi, "rho"], ["w"], col("w"), col(psi), Act.Copy, scale=col("rho"))
                op("t", ["ecol", "eye"], ["pe"], PE.matmul, T.pe[0:1, 0:128], T.ecol[:], T.eye[:], True, True)
                for c in ("u2", "u1", "u0"):
                    larger(c, "x16")
                for c in ("u2", "u1", "uo"):
                    act(["w"] + keys("x16", c), keys("x32", c), sb("x32", c), sb("x16", c), bias=-OFF, scale=col("w"))
                    if c != "uo":
                        store(c)
                ts(["w"] + keys("x16", "u0a"), keys("x32", "u0a"), sb("x32", "u0a"), sb("x16", "u0a"), col("w"), -OFF,
                   Op.mult, Op.add)
                store("u0")
                act([], ["pe", "erow"], T.erow[0:1, :], T.pe[0:1, 0:128], Act.Copy)
                op("s", ["erow"], [], S.dma_start, T.ye[:, 0], T.erow[0:1, :], dma="st")
                continue

            def plain(c, out):
                act(["rho"], [c] + keys(out, c), sb(out, c), ps(c), Act.Copy, scale=col("rho"))

            def level(q, c):
                if q == "s":
                    act(["w"] + keys("x16", c), keys("x32", c), sb("x32", c), sb("x16", c), Act.Copy, scale=col("w"))
                else:
                    ts(["w"] + keys("x16", c), keys("x32", c), sb("x32", c), sb("x16", c), col("w"), None, Op.mult)

            once = {"rr": lambda: spread("rr", ak(gain)[0], acc(gain), -1.0), "kk": own_key, "w": scale_after,
                    "side": lambda: side_by_side("rr", True), "min": least, "sel": choose,
                    "selu": lambda: ts(["sel", "w"], ["selu"], T.selu[:], T.sel[:], col("w"), 1 / S0, Op.mult, Op.mult),
                    "lay0": lambda: lay(0, "sel"), "lay1": lambda: lay(1, "selu"),
                    "own0": lambda: publish(t + 1, 0, 1 / S0)}
            for what, c in (x.split(":") for x in TURN):
                if what == "e":
                    once[c]()
                elif what == "g":
                    gather(c)
                elif what == "t":
                    after(c)
                elif what == "v":
                    ahead(c)
                elif what == "h":
                    larger(c, "x16") if c[0] == "u" else plain(c, "x16")
                elif what == "G":
                    pool_copy(c, "x32", "x16")
                elif c[0] == "b":
                    plain(c, "x32")
                else:
                    level(what.lower(), c)

    done = emit(g, T, ops, ext)
    g.sync.wait_ge(T.sem.st, done["st"])
    g.wait_ge(T.sem.sent, sent[0])
